import numpy as np
import ml_dtypes


def mxq(x, axis, fmt="e4m3"):
    dtype, down = {"e4m3": (ml_dtypes.float8_e4m3fn, 7), "e5m2": (ml_dtypes.float8_e5m2, 14)}[fmt]
    v = np.moveaxis(np.asarray(x, np.float32).astype(ml_dtypes.bfloat16).astype(np.float64), axis, -1)
    blocks = v.reshape(v.shape[:-1] + (-1, 32))
    amax = np.abs(blocks).max(-1, keepdims=True)
    byte = np.maximum(np.where(amax > 0, np.frexp(amax)[1] - 1 + 127, 0) - down, 1)
    scale = np.exp2(byte - 127.0)
    codes = (blocks / scale).astype(np.float32).astype(dtype).astype(np.float64)
    return np.moveaxis((codes * scale).reshape(v.shape), -1, axis)


WIDE = False


def mx_kscale(k):
    if not WIDE:
        return np.ones(k)
    levels = np.array([10, -10, 5, -5, 0])
    if k % 512:
        return np.exp2(np.random.permutation(np.resize(levels, k // 32))).repeat(32)
    a = np.empty((k // 512, 16))
    for p in range(k // 512):
        a[p, :8] = np.random.permutation(np.resize(levels, 8))
        for g in range(8):
            far = levels[np.abs(levels - a[p, g]) >= 10]
            a[p, g + 8] = far[np.random.randint(len(far))]
    return np.exp2(a.ravel()).repeat(32)


def f64(x):
    return np.asarray(x).astype(np.float64)


def striped(idx):
    return np.tile(idx.reshape(-1, 16).T, (8, 1)).astype(np.uint16)


def unstriped(offs):
    return offs[:16].T.reshape(-1).astype(np.int64)


def striped8(idx):
    return np.concatenate([x.reshape(-1, 16).T for x in idx]).astype(np.uint16)


def runs(offs, k):
    lists = np.stack([offs[16 * r : 16 * r + 16].T.reshape(-1) for r in range(8)]).astype(np.int64)
    return lists[np.arange(k) % 512 // 64]


def pack_weight(w):
    k, n = w.shape
    w = f64(np.asarray(w, np.float32).astype(ml_dtypes.bfloat16)).reshape(k // 32, 32, n)
    amax = np.abs(w).max(1)
    byte = np.clip(np.where(amax > 0, np.frexp(amax)[1] - 1 + 127 - 7, 1), 1, 254)
    scaled = (w * np.exp2(127.0 - byte)[:, None, :]).reshape(k, n).astype(np.float32)
    words = np.ascontiguousarray(scaled.reshape(k // 512, 128, 4, n).transpose(0, 1, 3, 2)).astype(ml_dtypes.float8_e4m3fn).view(np.uint8)
    return words, np.ascontiguousarray(byte.astype(np.uint8).reshape(k // 512, 16, n))


def unpack_weight(words, scales):
    g, p, n, _ = words.shape
    vals = np.ascontiguousarray(words).view(ml_dtypes.float8_e4m3fn).astype(np.float64) * np.repeat(np.exp2(scales.astype(np.float64) - 127.0), 8, axis=1)[..., None]
    return vals.transpose(0, 1, 3, 2).reshape(g * 512, n)


def sigmoid(v):
    return 1.0 / (1.0 + np.exp(-np.maximum(v, -700.0)))

def planes(y):
    n, m = y.shape
    v = y.astype(np.float32).astype(ml_dtypes.bfloat16).astype(np.float64).reshape(n // 32, 32, m)
    top = np.abs(v).max(1)
    byte = np.clip(np.where(top > 0, np.frexp(top)[1] - 1 + 127 - 7, 1), 1, 254)
    codes = (v * np.exp2(127.0 - byte)[:, None, :]).reshape(n, m).astype(np.float32).astype(ml_dtypes.float8_e4m3fn).view(np.uint8)
    words = codes.reshape(n // 512, 128, 4, m).transpose(0, 1, 3, 2)
    return np.ascontiguousarray(words), np.ascontiguousarray(byte.astype(np.uint8).reshape(n // 512, 16, m))


K, T, S, N = 1024, 2048, 512, 512


def setup_inputs():
    n = np.random.standard_normal
    s = mx_kscale(K)[:, None]
    packed_xT = pack_weight(n((K, T)) * s)
    return {
        "x_words": packed_xT[0],
        "x_scales": packed_xT[1],
        "w1": (n((K, N)) / np.sqrt(K) / s).astype(np.float32),
        "res1": np.random.uniform(0, 1, (N, S)).astype(np.float32),
        "res2": np.random.uniform(0, 1, (N, S)).astype(np.float32),
        "offs": striped(np.random.permutation(T)[:S]),
        "opp1": striped8(np.stack([np.random.permutation(S) for _ in range(8)])),
        "opp2": striped8(np.stack([np.random.permutation(S) for _ in range(8)])),
    }


def reference(x_words, x_scales, w1, res1, res2, offs, opp1, opp2):
    xq = unpack_weight(x_words, x_scales)[:, unstriped(offs)]
    y = mxq(f64(w1), 0, "e4m3").T @ xq
    out_0 = y + 0.75 * (f64(res1) - (sigmoid(y - (y[np.arange(N)[:, None], runs(opp1, N)]))) + f64(res2) - (sigmoid(y - (y[np.arange(N)[:, None], runs(opp2, N)]))))
    return (out_0,) + planes(out_0)

@@ -1,0 +1,197 @@
+from contextlib import ExitStack
+
+import concourse.mybir as mybir
+from concourse.masks import make_identity
+
+K, T, S, N = 1024, 2048, 512, 512
+FLOPS = 2 * K * S * N
+
+F32 = mybir.dt.float32
+BF16 = mybir.dt.bfloat16
+I32 = mybir.dt.int32
+U32 = mybir.dt.uint32
+U16 = mybir.dt.uint16
+U8 = mybir.dt.uint8
+FP8X4 = mybir.dt.float8_e4m3fn_x4
+ACT = mybir.ActivationFunctionType
+ALU = mybir.AluOpType
+
+P = 128
+PACK = 4
+PASSES = K // (P * PACK)
+BLK = 128
+BLOCKS = S // BLK
+HALF = S // 2
+CHUNKS = ((0, 256), (256, 384), (384, 512))
+
+
+def tile_picked_elo8_none_po_kernel(
+    tc, x_words, x_scales, w1, res1, res2, offs, opp1, opp2, out_0, out_1, out_2
+):
+    nc = tc.nc
+    with ExitStack() as ctx:
+        lists = ctx.enter_context(tc.tile_pool(name="lists", bufs=1))
+        keep = ctx.enter_context(tc.tile_pool(name="keep", bufs=1))
+        psum = ctx.enter_context(tc.psum_pool(name="psum", bufs=1))
+
+        offs_t = lists.tile([P, S // 16], U16, name="offs_t")
+        opp_t = [lists.tile([P, S // 16], U16, name="opp_t%d" % l) for l in range(2)]
+
+        warm_in = keep.tile([P, 1], F32, name="warm_in")
+        warm_out = keep.tile([P, 1], F32, name="warm_out")
+        nc.vector.memset(warm_in[:], 0.0)
+        nc.scalar.activation(out=warm_out[:], in_=warm_in[:], func=ACT.Sigmoid)
+
+        xs_raw = keep.tile([P, T], U8, name="xs_raw", align_bytes=64)
+        nc.gpsimd.memset(xs_raw[:].bitcast(I32), 0)
+        for q in range(4):
+            nc.gpsimd.dma_start(
+                out=xs_raw[32 * q : 32 * q + 8, :].bitcast(I32), in_=x_scales[:, 4 * q : 4 * q + 4, :].bitcast(I32)
+            )
+        ident = keep.tile([P, P], F32, name="ident")
+        make_identity(nc, ident[:])
+
+        xw_raw = [keep.tile([P, T], U32, name="xw_raw%d" % g, align_bytes=64) for g in range(PASSES)]
+        w_raw = [keep.tile([P, PACK, N], F32, name="w_raw%d" % g) for g in range(PASSES)]
+        w_rows = w1.rearrange("(g p j) c -> g p j c", p=P, j=PACK)
+
+        nc.sync.dma_start(out=w_raw[0][:], in_=w_rows[0])
+        nc.sync.dma_start(out=offs_t[:], in_=offs)
+        nc.sync.dma_start(out=w_raw[1][:], in_=w_rows[1])
+        for g in range(PASSES):
+            nc.sync.dma_start(
+                out=xw_raw[g][:].bitcast(I32), in_=x_words[g].rearrange("p n r -> p (n r)").bitcast(I32)
+            )
+        nc.sync.dma_start(out=opp_t[0][:], in_=opp1)
+        nc.sync.dma_start(out=opp_t[1][:], in_=opp2)
+        res_t = {}
+        for h in range(2):
+            for l, res in enumerate((res1, res2)):
+                res_t[l, h] = keep.tile([P, PACK, HALF], F32, name="res%d_%d" % (l, h))
+                nc.sync.dma_start(
+                    out=res_t[l, h][:],
+                    in_=res.rearrange("(p t) n -> p t n", t=PACK)[:, :, h * HALF : (h + 1) * HALF],
+                )
+
+        w_bf = [keep.tile([P, PACK * N], BF16, name="w_bf%d" % g, align_bytes=64) for g in range(PASSES)]
+        w_codes = [keep.tile([P, N], U32, name="w_codes%d" % g, align_bytes=64) for g in range(PASSES)]
+        w_sc = [keep.tile([P, N], U8, name="w_sc%d" % g, align_bytes=64) for g in range(PASSES)]
+        xw0 = keep.tile([P, S], U32, name="xw0", align_bytes=64)
+        xw1 = keep.tile([P, S], U32, name="xw1", align_bytes=64)
+        xw = [xw0, xw1]
+        xs = keep.tile([P, S], U8, name="xs", align_bytes=64)
+
+        def deal(copy, g, t0, t1):
+            copy(
+                out=w_bf[g][:].rearrange("p (t m j) -> p t m j", t=PACK, j=PACK)[:, t0:t1, :, :],
+                in_=w_raw[g][:].rearrange("p j (m t) -> p t m j", t=PACK)[:, t0:t1, :, :],
+            )
+
+        def quantize_w(g):
+            nc.vector.quantize_mx(out=w_codes[g][:].bitcast(FP8X4), scales=w_sc[g][:], in_=w_bf[g][:])
+
+        deal(nc.vector.tensor_copy, 0, 0, 2)
+        deal(nc.vector.tensor_copy, 0, 2, 3)
+        deal(nc.scalar.copy, 0, 3, 4)
+        nc.vector.tensor_copy(out=xs[:], in_=xs_raw[:].indirect(offs_t[:]))
+        quantize_w(0)
+        deal(nc.scalar.copy, 1, 0, 2)
+        deal(nc.vector.tensor_copy, 1, 2, 4)
+
+        parts = [(0, 0, HALF), (0, HALF, S)] + [(t, 0, S) for t in range(1, PACK)]
+        y_ps = [psum.tile([P, c1 - c0], F32, name="y_ps%d" % i, tag="bank%d" % i) for i, (t, c0, c1) in enumerate(parts)]
+
+        def product(g, i):
+            t, c0, c1 = parts[i]
+            nc.tensor.matmul_mx(
+                out=y_ps[i][:],
+                lhsT=w_codes[g][:, t * P : (t + 1) * P].bitcast(FP8X4),
+                lhsT_scale=w_sc[g][:, t * P : (t + 1) * P],
+                rhs=xw[g][:, c0:c1].bitcast(FP8X4),
+                rhs_scale=xs[4 * g : P, c0:c1],
+                start=(g == 0),
+                stop=(g == PASSES - 1),
+            )
+
+        nc.vector.tensor_copy(out=xw0[:], in_=xw_raw[0][:].indirect(offs_t[:]))
+        quantize_w(1)
+        for i in range(len(parts)):
+            product(0, i)
+        for h in range(2):
+            nc.vector.tensor_copy(
+                out=xw1[:, h * HALF : (h + 1) * HALF],
+                in_=xw_raw[1][:].indirect(offs_t[:, h * HALF // 16 : (h + 1) * HALF // 16]),
+            )
+
+        y_win = [keep.tile([P, S], F32, name="y_win%d" % t) for t in range(PACK)]
+        y_own = [keep.tile([P, PACK, HALF], F32, name="y_own%d" % h) for h in range(2)]
+        for i, (t, c0, c1) in enumerate(parts):
+            product(1, i)
+            nc.scalar.copy(out=y_win[t][:, c0:c1], in_=y_ps[i][:])
+            if c0 == 0:
+                nc.scalar.copy(out=y_own[0][:, t, :], in_=y_ps[i][:, 0:HALF])
+            if c1 == S:
+                nc.sync.dma_start(out=y_own[1][:, t, :], in_=y_win[t][:, HALF:S])
+
+        moves = []
+        for c, (c0, c1) in enumerate(CHUNKS):
+            h, r0 = divmod(c0, HALF)
+            width = c1 - c0
+            blocks = range(c0 // BLK, c1 // BLK)
+            sums = {b: psum.tile([P, PACK, P], F32, name="sums", tag="bank%d" % (4 + (b + 1) % 4)) for b in blocks}
+            for t in range(PACK):
+                slot = (c - 1, t + 2) if (c, t) == (len(CHUNKS) - 1, 0) else (c, t)
+                diff = keep.tile([P, 2, width], F32, name="diff", tag="diff%d_%d" % slot)
+                sig = keep.tile([P, 2, width], F32, name="sig%d_%d" % (c, t))
+                for l in range(2):
+                    nc.vector.tensor_tensor(
+                        out=diff[:, l, :],
+                        in0=y_win[t][:].indirect(opp_t[l][:, c0 // 16 : c1 // 16]),
+                        in1=y_own[h][:, t, r0 : r0 + width],
+                        op=ALU.subtract,
+                    )
+                nc.scalar.activation(out=sig[:], in_=diff[:], func=ACT.Sigmoid)
+                for b in blocks:
+                    s0 = b * BLK - c0
+                    terms = [res_t[l, h][:, t, r0 + s0 : r0 + s0 + BLK] for l in range(2)]
+                    terms.extend(sig[:, l, s0 : s0 + BLK] for l in range(2))
+                    for i, term in enumerate(terms):
+                        nc.tensor.matmul(
+                            out=sums[b][:, t, :],
+                            lhsT=term,
+                            rhs=ident[:],
+                            start=(i == 0),
+                            stop=(i == 3),
+                            is_transpose=True,
+                        )
+            for b in blocks:
+                move_t = keep.tile([P, PACK, P], F32, name="move_t%d" % b)
+                nc.scalar.activation(out=move_t[:], in_=sums[b][:], func=ACT.Copy, scale=0.75, bias=-1.5)
+                move = psum.tile([P, PACK, BLK], F32, name="move", tag="bank%d" % b)
+                for t in range(PACK):
+                    nc.tensor.transpose(move[:, t, :], move_t[:, t, :], ident[:])
+                moves.append(move)
+
+        o_codes = keep.tile([P, S], U32, name="o_codes", align_bytes=64)
+        o_sc = keep.tile([P, S], U8, name="o_sc", align_bytes=64)
+        out_rows = out_0.rearrange("(p t) n -> p t n", t=PACK)
+        out_words = out_1[0].rearrange("p n r -> p (n r)").bitcast(I32)
+        for b in range(BLOCKS):
+            h, r0 = divmod(b * BLK, HALF)
+            cols = slice(b * BLK, (b + 1) * BLK)
+            result = keep.tile([P, PACK, BLK], F32, name="result%d" % b)
+            nc.vector.tensor_tensor(out=result[:], in0=moves[b][:], in1=y_own[h][:, :, r0 : r0 + BLK], op=ALU.add)
+            nc.sync.dma_start(out=out_rows[:, :, cols], in_=result[:])
+            rounded = keep.tile([P, BLK * PACK], BF16, name="rounded%d" % b, align_bytes=64)
+            copy = nc.vector.tensor_copy if b == BLOCKS - 1 else nc.scalar.copy
+            copy(
+                out=rounded[:].rearrange("p (c i t) -> p c t i", i=4, t=PACK),
+                in_=result[:].rearrange("p t (c i) -> p c t i", i=4),
+            )
+            nc.vector.quantize_mx(out=o_codes[:, cols].bitcast(FP8X4), scales=o_sc[:, cols], in_=rounded[:])
+            nc.sync.dma_start(out=out_words[:, cols], in_=o_codes[:, cols].bitcast(I32))
+        for q in range(4):
+            queue = nc.scalar if q % 2 else nc.sync
+            queue.dma_start(
+                out=out_2[0, 4 * q : 4 * q + 4, :].bitcast(I32), in_=o_sc[32 * q : 32 * q + 4, :].bitcast(I32)
+            )

@@ -22,6 +22,7 @@ PASSES = K // (P * PACK)
 BLK = 128
 BLOCKS = S // BLK
 HALF = S // 2
+SIG_RING = 5
 CHUNKS = ((0, 256), (256, 384), (384, 512))
 
 
@@ -39,15 +40,11 @@ def tile_picked_elo8_none_po_kernel(
 
         warm_in = keep.tile([P, 1], F32, name="warm_in")
         warm_out = keep.tile([P, 1], F32, name="warm_out")
-        nc.vector.memset(warm_in[:], 0.0)
+        nc.gpsimd.memset(warm_in[:], 0.0)
         nc.scalar.activation(out=warm_out[:], in_=warm_in[:], func=ACT.Sigmoid)
 
         xs_raw = keep.tile([P, T], U8, name="xs_raw", align_bytes=64)
-        nc.gpsimd.memset(xs_raw[:].bitcast(I32), 0)
-        for q in range(4):
-            nc.gpsimd.dma_start(
-                out=xs_raw[32 * q : 32 * q + 8, :].bitcast(I32), in_=x_scales[:, 4 * q : 4 * q + 4, :].bitcast(I32)
-            )
+        nc.vector.memset(xs_raw[:].bitcast(I32), 0)
         ident = keep.tile([P, P], F32, name="ident")
         make_identity(nc, ident[:])
 
@@ -55,13 +52,20 @@ def tile_picked_elo8_none_po_kernel(
         w_raw = [keep.tile([P, PACK, N], F32, name="w_raw%d" % g) for g in range(PASSES)]
         w_rows = w1.rearrange("(g p j) c -> g p j c", p=P, j=PACK)
 
-        nc.sync.dma_start(out=w_raw[0][:], in_=w_rows[0])
-        nc.sync.dma_start(out=offs_t[:], in_=offs)
-        nc.sync.dma_start(out=w_raw[1][:], in_=w_rows[1])
-        for g in range(PASSES):
+        def load_words(g):
             nc.sync.dma_start(
                 out=xw_raw[g][:].bitcast(I32), in_=x_words[g].rearrange("p n r -> p (n r)").bitcast(I32)
             )
+
+        nc.sync.dma_start(out=offs_t[:], in_=offs)
+        nc.sync.dma_start(out=w_raw[0][:], in_=w_rows[0])
+        for q in range(4):
+            nc.sync.dma_start(
+                out=xs_raw[32 * q : 32 * q + 8, :].bitcast(I32), in_=x_scales[:, 4 * q : 4 * q + 4, :].bitcast(I32)
+            )
+        load_words(0)
+        nc.sync.dma_start(out=w_raw[1][:], in_=w_rows[1])
+        load_words(1)
         nc.sync.dma_start(out=opp_t[0][:], in_=opp1)
         nc.sync.dma_start(out=opp_t[1][:], in_=opp2)
         res_t = {}
@@ -90,13 +94,14 @@ def tile_picked_elo8_none_po_kernel(
         def quantize_w(g):
             nc.vector.quantize_mx(out=w_codes[g][:].bitcast(FP8X4), scales=w_sc[g][:], in_=w_bf[g][:])
 
-        deal(nc.vector.tensor_copy, 0, 0, 2)
-        deal(nc.vector.tensor_copy, 0, 2, 3)
-        deal(nc.scalar.copy, 0, 3, 4)
+        def prepare_w(g):
+            deal(nc.vector.tensor_copy, g, 0, 2)
+            deal(nc.vector.tensor_copy, g, 2, 3)
+            deal(nc.scalar.copy, g, 3, 4)
+            quantize_w(g)
+
+        prepare_w(0)
         nc.vector.tensor_copy(out=xs[:], in_=xs_raw[:].indirect(offs_t[:]))
-        quantize_w(0)
-        deal(nc.scalar.copy, 1, 0, 2)
-        deal(nc.vector.tensor_copy, 1, 2, 4)
 
         parts = [(0, 0, HALF), (0, HALF, S)] + [(t, 0, S) for t in range(1, PACK)]
         y_ps = [psum.tile([P, c1 - c0], F32, name="y_ps%d" % i, tag="bank%d" % i) for i, (t, c0, c1) in enumerate(parts)]
@@ -114,9 +119,9 @@ def tile_picked_elo8_none_po_kernel(
             )
 
         nc.vector.tensor_copy(out=xw0[:], in_=xw_raw[0][:].indirect(offs_t[:]))
-        quantize_w(1)
         for i in range(len(parts)):
             product(0, i)
+        prepare_w(1)
         for h in range(2):
             nc.vector.tensor_copy(
                 out=xw1[:, h * HALF : (h + 1) * HALF],
@@ -133,16 +138,26 @@ def tile_picked_elo8_none_po_kernel(
             if c1 == S:
                 nc.sync.dma_start(out=y_own[1][:, t, :], in_=y_win[t][:, HALF:S])
 
+        def add_turned(bank, t, term, start, stop):
+            nc.tensor.matmul(out=bank[:, t, :], lhsT=term, rhs=ident[:], start=start, stop=stop, is_transpose=True)
+
+        sums = []
+        for b in range(BLOCKS):
+            h, r0 = divmod(b * BLK, HALF)
+            sums.append(psum.tile([P, PACK, P], F32, name="sums", tag="bank%d" % ((5 + b) % 8)))
+            for l in range(2):
+                for t in range(PACK):
+                    add_turned(sums[b], t, res_t[l, h][:, t, r0 : r0 + BLK], (l, t) == (0, 0), False)
+
         moves = []
         for c, (c0, c1) in enumerate(CHUNKS):
             h, r0 = divmod(c0, HALF)
             width = c1 - c0
             blocks = range(c0 // BLK, c1 // BLK)
-            sums = {b: psum.tile([P, PACK, P], F32, name="sums", tag="bank%d" % (4 + (b + 1) % 4)) for b in blocks}
             for t in range(PACK):
                 slot = (c - 1, t + 2) if (c, t) == (len(CHUNKS) - 1, 0) else (c, t)
                 diff = keep.tile([P, 2, width], F32, name="diff", tag="diff%d_%d" % slot)
-                sig = keep.tile([P, 2, width], F32, name="sig%d_%d" % (c, t))
+                sig = keep.tile([P, 2, width], F32, name="sig", tag="sig%d" % ((PACK * c + t) % SIG_RING), align_bytes=64)
                 for l in range(2):
                     nc.vector.tensor_tensor(
                         out=diff[:, l, :],
@@ -153,21 +168,12 @@ def tile_picked_elo8_none_po_kernel(
                 nc.scalar.activation(out=sig[:], in_=diff[:], func=ACT.Sigmoid)
                 for b in blocks:
                     s0 = b * BLK - c0
-                    terms = [res_t[l, h][:, t, r0 + s0 : r0 + s0 + BLK] for l in range(2)]
-                    terms.extend(sig[:, l, s0 : s0 + BLK] for l in range(2))
-                    for i, term in enumerate(terms):
-                        nc.tensor.matmul(
-                            out=sums[b][:, t, :],
-                            lhsT=term,
-                            rhs=ident[:],
-                            start=(i == 0),
-                            stop=(i == 3),
-                            is_transpose=True,
-                        )
+                    for l in range(2):
+                        add_turned(sums[b], t, sig[:, l, s0 : s0 + BLK], False, (t, l) == (PACK - 1, 1))
             for b in blocks:
                 move_t = keep.tile([P, PACK, P], F32, name="move_t%d" % b)
                 nc.scalar.activation(out=move_t[:], in_=sums[b][:], func=ACT.Copy, scale=0.75, bias=-1.5)
-                move = psum.tile([P, PACK, BLK], F32, name="move", tag="bank%d" % b)
+                move = psum.tile([P, PACK, BLK], F32, name="move", tag="bank%d" % (1 + b))
                 for t in range(PACK):
                     nc.tensor.transpose(move[:, t, :], move_t[:, t, :], ident[:])
                 moves.append(move)
@@ -179,11 +185,12 @@ def tile_picked_elo8_none_po_kernel(
         for b in range(BLOCKS):
             h, r0 = divmod(b * BLK, HALF)
             cols = slice(b * BLK, (b + 1) * BLK)
-            result = keep.tile([P, PACK, BLK], F32, name="result%d" % b)
+            result = keep.tile([P, PACK, BLK], F32, name="result", tag="diff%d_%d" % (len(CHUNKS) - 1, b + 1))
             nc.vector.tensor_tensor(out=result[:], in0=moves[b][:], in1=y_own[h][:, :, r0 : r0 + BLK], op=ALU.add)
             nc.sync.dma_start(out=out_rows[:, :, cols], in_=result[:])
-            rounded = keep.tile([P, BLK * PACK], BF16, name="rounded%d" % b, align_bytes=64)
-            copy = nc.vector.tensor_copy if b == BLOCKS - 1 else nc.scalar.copy
+            slot = "sig%d" % ((PACK * len(CHUNKS) - 1) % SIG_RING) if b == 1 else "rounded%d" % b
+            rounded = keep.tile([P, BLK * PACK], BF16, name="rounded", tag=slot, align_bytes=64)
+            copy = nc.scalar.copy if b in (1, 2) else nc.vector.tensor_copy
             copy(
                 out=rounded[:].rearrange("p (c i t) -> p c t i", i=4, t=PACK),
                 in_=result[:].rearrange("p t (c i) -> p c t i", i=4),

@@ -22,8 +22,7 @@ PASSES = K // (P * PACK)
 BLK = 128
 BLOCKS = S // BLK
 HALF = S // 2
-SIG_RING = 5
-CHUNKS = ((0, 256), (256, 384), (384, 512))
+DEAL_SPLIT = 84
 
 
 def tile_picked_elo8_none_po_kernel(
@@ -52,53 +51,40 @@ def tile_picked_elo8_none_po_kernel(
         w_raw = [keep.tile([P, PACK, N], F32, name="w_raw%d" % g) for g in range(PASSES)]
         w_rows = w1.rearrange("(g p j) c -> g p j c", p=P, j=PACK)
 
-        def load_words(g):
-            nc.sync.dma_start(
-                out=xw_raw[g][:].bitcast(I32), in_=x_words[g].rearrange("p n r -> p (n r)").bitcast(I32)
-            )
-
         nc.sync.dma_start(out=offs_t[:], in_=offs)
         nc.sync.dma_start(out=w_raw[0][:], in_=w_rows[0])
         for q in range(4):
             nc.sync.dma_start(
                 out=xs_raw[32 * q : 32 * q + 8, :].bitcast(I32), in_=x_scales[:, 4 * q : 4 * q + 4, :].bitcast(I32)
             )
-        load_words(0)
+        word_rows = [x_words[g].rearrange("p n r -> p (n r)").bitcast(I32) for g in range(PASSES)]
+        nc.sync.dma_start(out=xw_raw[0][:].bitcast(I32), in_=word_rows[0])
         nc.sync.dma_start(out=w_raw[1][:], in_=w_rows[1])
-        load_words(1)
+        nc.sync.dma_start(out=xw_raw[1][:].bitcast(I32), in_=word_rows[1])
         nc.sync.dma_start(out=opp_t[0][:], in_=opp1)
         nc.sync.dma_start(out=opp_t[1][:], in_=opp2)
-        res_t = {}
-        for h in range(2):
-            for l, res in enumerate((res1, res2)):
-                res_t[l, h] = keep.tile([P, PACK, HALF], F32, name="res%d_%d" % (l, h))
-                nc.sync.dma_start(
-                    out=res_t[l, h][:],
-                    in_=res.rearrange("(p t) n -> p t n", t=PACK)[:, :, h * HALF : (h + 1) * HALF],
-                )
+        res_rows = [res.rearrange("(p t) n -> p t n", t=PACK) for res in (res1, res2)]
+        res_late = {}
+        for u in range(2):
+            for l in range(2):
+                res_late[l, u] = keep.tile([P, 2, HALF], F32, name="res_late%d_%d" % (l, u))
+                nc.sync.dma_start(out=res_late[l, u][:], in_=res_rows[l][:, 2 * u : 2 * u + 2, HALF:S])
+        res_early = [keep.tile([P, PACK, HALF], F32, name="res_early%d" % l) for l in range(2)]
+        for l in range(2):
+            nc.sync.dma_start(out=res_early[l][:], in_=res_rows[l][:, :, 0:HALF])
 
         w_bf = [keep.tile([P, PACK * N], BF16, name="w_bf%d" % g, align_bytes=64) for g in range(PASSES)]
         w_codes = [keep.tile([P, N], U32, name="w_codes%d" % g, align_bytes=64) for g in range(PASSES)]
         w_sc = [keep.tile([P, N], U8, name="w_sc%d" % g, align_bytes=64) for g in range(PASSES)]
-        xw0 = keep.tile([P, S], U32, name="xw0", align_bytes=64)
-        xw1 = keep.tile([P, S], U32, name="xw1", align_bytes=64)
-        xw = [xw0, xw1]
+        xw = [keep.tile([P, S], U32, name="xw%d" % g, align_bytes=64) for g in range(PASSES)]
         xs = keep.tile([P, S], U8, name="xs", align_bytes=64)
 
-        def deal(copy, g, t0, t1):
-            copy(
-                out=w_bf[g][:].rearrange("p (t m j) -> p t m j", t=PACK, j=PACK)[:, t0:t1, :, :],
-                in_=w_raw[g][:].rearrange("p j (m t) -> p t m j", t=PACK)[:, t0:t1, :, :],
-            )
-
-        def quantize_w(g):
-            nc.vector.quantize_mx(out=w_codes[g][:].bitcast(FP8X4), scales=w_sc[g][:], in_=w_bf[g][:])
-
         def prepare_w(g):
-            deal(nc.vector.tensor_copy, g, 0, 2)
-            deal(nc.vector.tensor_copy, g, 2, 3)
-            deal(nc.scalar.copy, g, 3, 4)
-            quantize_w(g)
+            dealt = w_bf[g][:].rearrange("p (t m j) -> p m j t", t=PACK, j=PACK)
+            source = w_raw[g][:].rearrange("p j (m t) -> p m j t", t=PACK)
+            nc.vector.tensor_copy(out=dealt[:, 0:DEAL_SPLIT, :, :], in_=source[:, 0:DEAL_SPLIT, :, :])
+            nc.scalar.copy(out=dealt[:, DEAL_SPLIT:P, :, :], in_=source[:, DEAL_SPLIT:P, :, :])
+            nc.vector.quantize_mx(out=w_codes[g][:].bitcast(FP8X4), scales=w_sc[g][:], in_=w_bf[g][:])
 
         prepare_w(0)
         nc.vector.tensor_copy(out=xs[:], in_=xs_raw[:].indirect(offs_t[:]))
@@ -118,14 +104,20 @@ def tile_picked_elo8_none_po_kernel(
                 stop=(g == PASSES - 1),
             )
 
-        nc.vector.tensor_copy(out=xw0[:], in_=xw_raw[0][:].indirect(offs_t[:]))
+        nc.vector.tensor_copy(out=xw[0][:], in_=xw_raw[0][:].indirect(offs_t[:]))
         for i in range(len(parts)):
             product(0, i)
         prepare_w(1)
         for h in range(2):
             nc.vector.tensor_copy(
-                out=xw1[:, h * HALF : (h + 1) * HALF],
+                out=xw[1][:, h * HALF : (h + 1) * HALF],
                 in_=xw_raw[1][:].indirect(offs_t[:, h * HALF // 16 : (h + 1) * HALF // 16]),
+            )
+
+        res_sum = keep.tile([P, PACK, HALF], F32, name="res_sum")
+        for u in range(2):
+            nc.vector.tensor_tensor(
+                out=res_sum[:, 2 * u : 2 * u + 2, :], in0=res_late[0, u][:], in1=res_late[1, u][:], op=ALU.add
             )
 
         y_win = [keep.tile([P, S], F32, name="y_win%d" % t) for t in range(PACK)]
@@ -135,68 +127,95 @@ def tile_picked_elo8_none_po_kernel(
             nc.scalar.copy(out=y_win[t][:, c0:c1], in_=y_ps[i][:])
             if c0 == 0:
                 nc.scalar.copy(out=y_own[0][:, t, :], in_=y_ps[i][:, 0:HALF])
+        for i, (t, c0, c1) in enumerate(parts):
             if c1 == S:
-                nc.sync.dma_start(out=y_own[1][:, t, :], in_=y_win[t][:, HALF:S])
+                nc.scalar.copy(out=y_own[1][:, t, :], in_=y_ps[i][:, HALF - c0 : S - c0])
+
+        def differences(h, t):
+            diff = keep.tile([P, 2, HALF], F32, name="diff%d_%d" % (h, t))
+            for l in range(2):
+                nc.vector.tensor_tensor(
+                    out=diff[:, l, :],
+                    in0=y_win[t][:].indirect(opp_t[l][:, h * HALF // 16 : (h + 1) * HALF // 16]),
+                    in1=y_own[h][:, t, :],
+                    op=ALU.subtract,
+                )
+            return diff
 
         def add_turned(bank, t, term, start, stop):
             nc.tensor.matmul(out=bank[:, t, :], lhsT=term, rhs=ident[:], start=start, stop=stop, is_transpose=True)
 
-        sums = []
-        for b in range(BLOCKS):
-            h, r0 = divmod(b * BLK, HALF)
-            sums.append(psum.tile([P, PACK, P], F32, name="sums", tag="bank%d" % ((5 + b) % 8)))
-            for l in range(2):
+        early_blocks = range(HALF // BLK)
+        sums = [psum.tile([P, PACK, P], F32, name="sums", tag="bank%d" % (5 + b)) for b in early_blocks]
+        for l in range(2):
+            for b in early_blocks:
                 for t in range(PACK):
-                    add_turned(sums[b], t, res_t[l, h][:, t, r0 : r0 + BLK], (l, t) == (0, 0), False)
-
-        moves = []
-        for c, (c0, c1) in enumerate(CHUNKS):
-            h, r0 = divmod(c0, HALF)
-            width = c1 - c0
-            blocks = range(c0 // BLK, c1 // BLK)
-            for t in range(PACK):
-                slot = (c - 1, t + 2) if (c, t) == (len(CHUNKS) - 1, 0) else (c, t)
-                diff = keep.tile([P, 2, width], F32, name="diff", tag="diff%d_%d" % slot)
-                sig = keep.tile([P, 2, width], F32, name="sig", tag="sig%d" % ((PACK * c + t) % SIG_RING), align_bytes=64)
+                    add_turned(sums[b], t, res_early[l][:, t, b * BLK : (b + 1) * BLK], (l, t) == (0, 0), False)
+        for t in range(PACK):
+            diff = differences(0, t)
+            lose = keep.tile([P, 2, HALF], F32, name="lose%d" % t)
+            nc.scalar.activation(out=lose[:], in_=diff[:], func=ACT.Sigmoid)
+            for b in early_blocks:
                 for l in range(2):
-                    nc.vector.tensor_tensor(
-                        out=diff[:, l, :],
-                        in0=y_win[t][:].indirect(opp_t[l][:, c0 // 16 : c1 // 16]),
-                        in1=y_own[h][:, t, r0 : r0 + width],
-                        op=ALU.subtract,
-                    )
-                nc.scalar.activation(out=sig[:], in_=diff[:], func=ACT.Sigmoid)
-                for b in blocks:
-                    s0 = b * BLK - c0
-                    for l in range(2):
-                        add_turned(sums[b], t, sig[:, l, s0 : s0 + BLK], False, (t, l) == (PACK - 1, 1))
-            for b in blocks:
-                move_t = keep.tile([P, PACK, P], F32, name="move_t%d" % b)
-                nc.scalar.activation(out=move_t[:], in_=sums[b][:], func=ACT.Copy, scale=0.75, bias=-1.5)
-                move = psum.tile([P, PACK, BLK], F32, name="move", tag="bank%d" % (1 + b))
-                for t in range(PACK):
-                    nc.tensor.transpose(move[:, t, :], move_t[:, t, :], ident[:])
-                moves.append(move)
+                    add_turned(sums[b], t, lose[:, l, b * BLK : (b + 1) * BLK], False, (t, l) == (PACK - 1, 1))
+        late_diffs = [differences(1, t) for t in range(PACK)]
+        moves = []
+        for b in early_blocks:
+            move_t = keep.tile([P, PACK, P], F32, name="move_t%d" % b)
+            nc.scalar.activation(out=move_t[:], in_=sums[b][:], func=ACT.Copy, scale=0.75, bias=-1.5)
+            move = psum.tile([P, PACK, BLK], F32, name="move", tag="bank%d" % (7 * (1 - b)))
+            for t in range(PACK):
+                nc.tensor.transpose(move[:, t, :], move_t[:, t, :], ident[:])
+            moves.append(move)
 
         o_codes = keep.tile([P, S], U32, name="o_codes", align_bytes=64)
         o_sc = keep.tile([P, S], U8, name="o_sc", align_bytes=64)
         out_rows = out_0.rearrange("(p t) n -> p t n", t=PACK)
         out_words = out_1[0].rearrange("p n r -> p (n r)").bitcast(I32)
-        for b in range(BLOCKS):
-            h, r0 = divmod(b * BLK, HALF)
-            cols = slice(b * BLK, (b + 1) * BLK)
-            result = keep.tile([P, PACK, BLK], F32, name="result", tag="diff%d_%d" % (len(CHUNKS) - 1, b + 1))
-            nc.vector.tensor_tensor(out=result[:], in0=moves[b][:], in1=y_own[h][:, :, r0 : r0 + BLK], op=ALU.add)
-            nc.sync.dma_start(out=out_rows[:, :, cols], in_=result[:])
-            slot = "sig%d" % ((PACK * len(CHUNKS) - 1) % SIG_RING) if b == 1 else "rounded%d" % b
-            rounded = keep.tile([P, BLK * PACK], BF16, name="rounded", tag=slot, align_bytes=64)
-            copy = nc.scalar.copy if b in (1, 2) else nc.vector.tensor_copy
+        rounded = [keep.tile([P, HALF * PACK], BF16, name="rounded%d" % h, align_bytes=64) for h in range(2)]
+
+        def round_columns(copy, h, result, r0, r1):
             copy(
-                out=rounded[:].rearrange("p (c i t) -> p c t i", i=4, t=PACK),
-                in_=result[:].rearrange("p t (c i) -> p c t i", i=4),
+                out=rounded[h][:, r0 * PACK : r1 * PACK].rearrange("p (c i t) -> p c t i", i=4, t=PACK),
+                in_=result.rearrange("p t (c i) -> p c t i", i=4),
             )
-            nc.vector.quantize_mx(out=o_codes[:, cols].bitcast(FP8X4), scales=o_sc[:, cols], in_=rounded[:])
+
+        def quantize_half(h):
+            cols = slice(h * HALF, (h + 1) * HALF)
+            nc.vector.quantize_mx(out=o_codes[:, cols].bitcast(FP8X4), scales=o_sc[:, cols], in_=rounded[h][:])
             nc.sync.dma_start(out=out_words[:, cols], in_=o_codes[:, cols].bitcast(I32))
+
+        win = keep.tile([P, 2, PACK, HALF], F32, name="win")
+        for t in range(PACK):
+            nc.scalar.activation(out=win[:, :, t, :], in_=late_diffs[t][:], func=ACT.Sigmoid, scale=-1.0)
+        stages = [keep.tile([P, PACK, HALF], F32, name="stage%d" % i) for i in range(3)]
+        blocks = [slice(b * BLK, (b + 1) * BLK) for b in early_blocks]
+        terms = [(res_sum[:], 0.75), (win[:, 0, :, :], -0.75), (win[:, 1, :, :], -0.75)]
+        for i, (term, factor) in enumerate(terms):
+            before = stages[i - 1] if i else y_own[1]
+            for cols in blocks:
+                nc.vector.scalar_tensor_tensor(
+                    out=stages[i][:, :, cols],
+                    in0=term[:, :, cols],
+                    scalar=factor,
+                    in1=before[:, :, cols],
+                    op0=ALU.mult,
+                    op1=ALU.add,
+                )
+        late = stages[2]
+        nc.sync.dma_start(out=out_rows[:, :, HALF:S], in_=late[:])
+        for cols in blocks:
+            round_columns(nc.scalar.copy, 1, late[:, :, cols], cols.start, cols.stop)
+        results = []
+        for b, cols in enumerate(blocks):
+            result = keep.tile([P, PACK, BLK], F32, name="result%d" % b)
+            nc.vector.tensor_tensor(out=result[:], in0=moves[b][:], in1=y_own[0][:, :, cols], op=ALU.add)
+            nc.sync.dma_start(out=out_rows[:, :, cols], in_=result[:])
+            results.append(result)
+        round_columns(nc.scalar.copy, 0, results[0][:], 0, BLK)
+        quantize_half(1)
+        round_columns(nc.vector.tensor_copy, 0, results[1][:], BLK, HALF)
+        quantize_half(0)
         for q in range(4):
             queue = nc.scalar if q % 2 else nc.sync
             queue.dma_start(

@@ -37,11 +37,6 @@ def tile_picked_elo8_none_po_kernel(
         offs_t = lists.tile([P, S // 16], U16, name="offs_t")
         opp_t = [lists.tile([P, S // 16], U16, name="opp_t%d" % l) for l in range(2)]
 
-        warm_in = keep.tile([P, 1], F32, name="warm_in")
-        warm_out = keep.tile([P, 1], F32, name="warm_out")
-        nc.gpsimd.memset(warm_in[:], 0.0)
-        nc.scalar.activation(out=warm_out[:], in_=warm_in[:], func=ACT.Sigmoid)
-
         xs_raw = keep.tile([P, T], U8, name="xs_raw", align_bytes=64)
         nc.vector.memset(xs_raw[:].bitcast(I32), 0)
         ident = keep.tile([P, P], F32, name="ident")
@@ -51,17 +46,24 @@ def tile_picked_elo8_none_po_kernel(
         w_raw = [keep.tile([P, PACK, N], F32, name="w_raw%d" % g) for g in range(PASSES)]
         w_rows = w1.rearrange("(g p j) c -> g p j c", p=P, j=PACK)
 
-        nc.sync.dma_start(out=offs_t[:], in_=offs)
-        nc.sync.dma_start(out=w_raw[0][:], in_=w_rows[0])
-        for q in range(4):
-            nc.sync.dma_start(
-                out=xs_raw[32 * q : 32 * q + 8, :].bitcast(I32), in_=x_scales[:, 4 * q : 4 * q + 4, :].bitcast(I32)
-            )
         word_rows = [x_words[g].rearrange("p n r -> p (n r)").bitcast(I32) for g in range(PASSES)]
+
+        def load_scales(first, last):
+            for i in range(first, last):
+                g, q = divmod(i, 4)
+                nc.sync.dma_start(
+                    out=xs_raw[32 * q + 4 * g : 32 * q + 4 * g + 4, :].bitcast(I32),
+                    in_=x_scales[g, 4 * q : 4 * q + 4, :].bitcast(I32),
+                )
+
+        nc.sync.dma_start(out=offs_t[:], in_=offs)
+        nc.sync.dma_start(out=opp_t[0][:], in_=opp1)
+        nc.sync.dma_start(out=w_raw[0][:], in_=w_rows[0])
+        load_scales(0, 6)
         nc.sync.dma_start(out=xw_raw[0][:].bitcast(I32), in_=word_rows[0])
+        load_scales(6, 8)
         nc.sync.dma_start(out=w_raw[1][:], in_=w_rows[1])
         nc.sync.dma_start(out=xw_raw[1][:].bitcast(I32), in_=word_rows[1])
-        nc.sync.dma_start(out=opp_t[0][:], in_=opp1)
         nc.sync.dma_start(out=opp_t[1][:], in_=opp2)
         res_rows = [res.rearrange("(p t) n -> p t n", t=PACK) for res in (res1, res2)]
         res_late = {}
@@ -80,14 +82,13 @@ def tile_picked_elo8_none_po_kernel(
         xs = keep.tile([P, S], U8, name="xs", align_bytes=64)
 
         def prepare_w(g):
-            dealt = w_bf[g][:].rearrange("p (t m j) -> p m j t", t=PACK, j=PACK)
-            source = w_raw[g][:].rearrange("p j (m t) -> p m j t", t=PACK)
+            dealt = w_bf[g][:].rearrange("p (t m j) -> p m t j", t=PACK, j=PACK)
+            source = w_raw[g][:].rearrange("p j (m t) -> p m t j", t=PACK)
             nc.vector.tensor_copy(out=dealt[:, 0:DEAL_SPLIT, :, :], in_=source[:, 0:DEAL_SPLIT, :, :])
             nc.scalar.copy(out=dealt[:, DEAL_SPLIT:P, :, :], in_=source[:, DEAL_SPLIT:P, :, :])
             nc.vector.quantize_mx(out=w_codes[g][:].bitcast(FP8X4), scales=w_sc[g][:], in_=w_bf[g][:])
 
         prepare_w(0)
-        nc.vector.tensor_copy(out=xs[:], in_=xs_raw[:].indirect(offs_t[:]))
 
         parts = [(0, 0, HALF), (0, HALF, S)] + [(t, 0, S) for t in range(1, PACK)]
         y_ps = [psum.tile([P, c1 - c0], F32, name="y_ps%d" % i, tag="bank%d" % i) for i, (t, c0, c1) in enumerate(parts)]
@@ -105,6 +106,7 @@ def tile_picked_elo8_none_po_kernel(
             )
 
         nc.vector.tensor_copy(out=xw[0][:], in_=xw_raw[0][:].indirect(offs_t[:]))
+        nc.vector.tensor_copy(out=xs[:], in_=xs_raw[:].indirect(offs_t[:]))
         for i in range(len(parts)):
             product(0, i)
         prepare_w(1)

@@ -19,10 +19,18 @@ ALU = mybir.AluOpType
 P = 128
 PACK = 4
 PASSES = K // (P * PACK)
+QUADS = 4
+SCALE_ROWS = 4
+GROUP = 16
+GAMES = 2
 BLK = 128
 BLOCKS = S // BLK
 HALF = S // 2
+STEP = 0.75
 DEAL_SPLIT = 84
+CHUNKS = ((0, HALF), (HALF, HALF + BLK), (HALF + BLK, S))
+TURNED = 3
+SCALES_FIRST = 6
 
 
 def tile_picked_elo8_none_po_kernel(
@@ -34,8 +42,8 @@ def tile_picked_elo8_none_po_kernel(
         keep = ctx.enter_context(tc.tile_pool(name="keep", bufs=1))
         psum = ctx.enter_context(tc.psum_pool(name="psum", bufs=1))
 
-        offs_t = lists.tile([P, S // 16], U16, name="offs_t")
-        opp_t = [lists.tile([P, S // 16], U16, name="opp_t%d" % l) for l in range(2)]
+        offs_t = lists.tile([P, S // GROUP], U16, name="offs_t")
+        opp_t = [lists.tile([P, S // GROUP], U16, name="opp_t%d" % l) for l in range(GAMES)]
 
         xs_raw = keep.tile([P, T], U8, name="xs_raw", align_bytes=64)
         nc.vector.memset(xs_raw[:].bitcast(I32), 0)
@@ -45,34 +53,34 @@ def tile_picked_elo8_none_po_kernel(
         xw_raw = [keep.tile([P, T], U32, name="xw_raw%d" % g, align_bytes=64) for g in range(PASSES)]
         w_raw = [keep.tile([P, PACK, N], F32, name="w_raw%d" % g) for g in range(PASSES)]
         w_rows = w1.rearrange("(g p j) c -> g p j c", p=P, j=PACK)
-
         word_rows = [x_words[g].rearrange("p n r -> p (n r)").bitcast(I32) for g in range(PASSES)]
 
         def load_scales(first, last):
             for i in range(first, last):
-                g, q = divmod(i, 4)
+                g, q = divmod(i, QUADS)
+                row = 32 * q + SCALE_ROWS * g
                 nc.sync.dma_start(
-                    out=xs_raw[32 * q + 4 * g : 32 * q + 4 * g + 4, :].bitcast(I32),
-                    in_=x_scales[g, 4 * q : 4 * q + 4, :].bitcast(I32),
+                    out=xs_raw[row : row + SCALE_ROWS, :].bitcast(I32),
+                    in_=x_scales[g, SCALE_ROWS * q : SCALE_ROWS * (q + 1), :].bitcast(I32),
                 )
 
         nc.sync.dma_start(out=offs_t[:], in_=offs)
         nc.sync.dma_start(out=opp_t[0][:], in_=opp1)
         nc.sync.dma_start(out=w_raw[0][:], in_=w_rows[0])
-        load_scales(0, 6)
+        load_scales(0, SCALES_FIRST)
         nc.sync.dma_start(out=xw_raw[0][:].bitcast(I32), in_=word_rows[0])
-        load_scales(6, 8)
+        load_scales(SCALES_FIRST, PASSES * QUADS)
         nc.sync.dma_start(out=w_raw[1][:], in_=w_rows[1])
         nc.sync.dma_start(out=xw_raw[1][:].bitcast(I32), in_=word_rows[1])
         nc.sync.dma_start(out=opp_t[1][:], in_=opp2)
         res_rows = [res.rearrange("(p t) n -> p t n", t=PACK) for res in (res1, res2)]
         res_late = {}
-        for u in range(2):
-            for l in range(2):
+        for u in range(PACK // 2):
+            for l in range(GAMES):
                 res_late[l, u] = keep.tile([P, 2, HALF], F32, name="res_late%d_%d" % (l, u))
                 nc.sync.dma_start(out=res_late[l, u][:], in_=res_rows[l][:, 2 * u : 2 * u + 2, HALF:S])
-        res_early = [keep.tile([P, PACK, HALF], F32, name="res_early%d" % l) for l in range(2)]
-        for l in range(2):
+        res_early = [keep.tile([P, PACK, HALF], F32, name="res_early%d" % l) for l in range(GAMES)]
+        for l in range(GAMES):
             nc.sync.dma_start(out=res_early[l][:], in_=res_rows[l][:, :, 0:HALF])
 
         w_bf = [keep.tile([P, PACK * N], BF16, name="w_bf%d" % g, align_bytes=64) for g in range(PASSES)]
@@ -100,7 +108,7 @@ def tile_picked_elo8_none_po_kernel(
                 lhsT=w_codes[g][:, t * P : (t + 1) * P].bitcast(FP8X4),
                 lhsT_scale=w_sc[g][:, t * P : (t + 1) * P],
                 rhs=xw[g][:, c0:c1].bitcast(FP8X4),
-                rhs_scale=xs[4 * g : P, c0:c1],
+                rhs_scale=xs[SCALE_ROWS * g : P, c0:c1],
                 start=(g == 0),
                 stop=(g == PASSES - 1),
             )
@@ -113,62 +121,70 @@ def tile_picked_elo8_none_po_kernel(
         for h in range(2):
             nc.vector.tensor_copy(
                 out=xw[1][:, h * HALF : (h + 1) * HALF],
-                in_=xw_raw[1][:].indirect(offs_t[:, h * HALF // 16 : (h + 1) * HALF // 16]),
+                in_=xw_raw[1][:].indirect(offs_t[:, h * HALF // GROUP : (h + 1) * HALF // GROUP]),
             )
 
         res_sum = keep.tile([P, PACK, HALF], F32, name="res_sum")
-        for u in range(2):
-            nc.vector.tensor_tensor(
-                out=res_sum[:, 2 * u : 2 * u + 2, :], in0=res_late[0, u][:], in1=res_late[1, u][:], op=ALU.add
+        for u in range(PACK // 2):
+            nc.vector.scalar_tensor_tensor(
+                out=res_sum[:, 2 * u : 2 * u + 2, :],
+                in0=res_late[0, u][:],
+                scalar=-float(GAMES),
+                in1=res_late[1, u][:],
+                op0=ALU.add,
+                op1=ALU.add,
             )
 
         y_win = [keep.tile([P, S], F32, name="y_win%d" % t) for t in range(PACK)]
-        y_own = [keep.tile([P, PACK, HALF], F32, name="y_own%d" % h) for h in range(2)]
+        y_own = [keep.tile([P, PACK, c1 - c0], F32, name="y_own%d" % c) for c, (c0, c1) in enumerate(CHUNKS)]
         for i, (t, c0, c1) in enumerate(parts):
             product(1, i)
             nc.scalar.copy(out=y_win[t][:, c0:c1], in_=y_ps[i][:])
             if c0 == 0:
                 nc.scalar.copy(out=y_own[0][:, t, :], in_=y_ps[i][:, 0:HALF])
-        for i, (t, c0, c1) in enumerate(parts):
-            if c1 == S:
-                nc.scalar.copy(out=y_own[1][:, t, :], in_=y_ps[i][:, HALF - c0 : S - c0])
-
-        def differences(h, t):
-            diff = keep.tile([P, 2, HALF], F32, name="diff%d_%d" % (h, t))
-            for l in range(2):
-                nc.vector.tensor_tensor(
-                    out=diff[:, l, :],
-                    in0=y_win[t][:].indirect(opp_t[l][:, h * HALF // 16 : (h + 1) * HALF // 16]),
-                    in1=y_own[h][:, t, :],
-                    op=ALU.subtract,
-                )
-            return diff
+        for c in range(1, len(CHUNKS)):
+            for t in range(PACK):
+                nc.sync.dma_start(out=y_own[c][:, t, :], in_=y_win[t][:, CHUNKS[c][0] : CHUNKS[c][1]])
 
         def add_turned(bank, t, term, start, stop):
             nc.tensor.matmul(out=bank[:, t, :], lhsT=term, rhs=ident[:], start=start, stop=stop, is_transpose=True)
 
-        early_blocks = range(HALF // BLK)
-        sums = [psum.tile([P, PACK, P], F32, name="sums", tag="bank%d" % (5 + b)) for b in early_blocks]
-        for l in range(2):
-            for b in early_blocks:
+        sums = [psum.tile([P, PACK, P], F32, name="sums", tag="bank%d" % (len(parts) + b)) for b in range(TURNED)]
+        early_blocks = HALF // BLK
+        for l in range(GAMES):
+            for b in range(early_blocks):
                 for t in range(PACK):
                     add_turned(sums[b], t, res_early[l][:, t, b * BLK : (b + 1) * BLK], (l, t) == (0, 0), False)
         for t in range(PACK):
-            diff = differences(0, t)
-            lose = keep.tile([P, 2, HALF], F32, name="lose%d" % t)
-            nc.scalar.activation(out=lose[:], in_=diff[:], func=ACT.Sigmoid)
-            for b in early_blocks:
-                for l in range(2):
-                    add_turned(sums[b], t, lose[:, l, b * BLK : (b + 1) * BLK], False, (t, l) == (PACK - 1, 1))
-        late_diffs = [differences(1, t) for t in range(PACK)]
+            add_turned(sums[early_blocks], t, res_sum[:, t, 0:BLK], t == 0, False)
+
+        sig = []
         moves = []
-        for b in early_blocks:
-            move_t = keep.tile([P, PACK, P], F32, name="move_t%d" % b)
-            nc.scalar.activation(out=move_t[:], in_=sums[b][:], func=ACT.Copy, scale=0.75, bias=-1.5)
-            move = psum.tile([P, PACK, BLK], F32, name="move", tag="bank%d" % (7 * (1 - b)))
+        for c, (c0, c1) in enumerate(CHUNKS):
+            sig.append(keep.tile([P, GAMES, PACK, c1 - c0], F32, name="sig%d" % c))
+            blocks = [b for b in range(c0 // BLK, c1 // BLK) if b < TURNED]
             for t in range(PACK):
-                nc.tensor.transpose(move[:, t, :], move_t[:, t, :], ident[:])
-            moves.append(move)
+                diff = keep.tile([P, GAMES, c1 - c0], F32, name="diff", tag="diff%d_%d" % (c, t))
+                for l in range(GAMES):
+                    nc.vector.tensor_tensor(
+                        out=diff[:, l, :],
+                        in0=y_win[t][:].indirect(opp_t[l][:, c0 // GROUP : c1 // GROUP]),
+                        in1=y_own[c][:, t, :],
+                        op=ALU.subtract,
+                    )
+                nc.scalar.activation(out=sig[c][:, :, t, :], in_=diff[:], func=ACT.Sigmoid)
+                for b in blocks:
+                    for l in range(GAMES):
+                        term = sig[c][:, l, t, b * BLK - c0 : (b + 1) * BLK - c0]
+                        add_turned(sums[b], t, term, False, (t, l) == (PACK - 1, GAMES - 1))
+            for b in blocks:
+                move_t = keep.tile([P, PACK, P], F32, name="move_t%d" % b)
+                bias = -STEP * GAMES if b < early_blocks else 0.0
+                nc.scalar.activation(out=move_t[:], in_=sums[b][:], func=ACT.Copy, scale=STEP, bias=bias)
+                move = psum.tile([P, PACK, BLK], F32, name="move", tag="bank%d" % b)
+                for t in range(PACK):
+                    nc.tensor.transpose(move[:, t, :], move_t[:, t, :], ident[:])
+                moves.append(move)
 
         o_codes = keep.tile([P, S], U32, name="o_codes", align_bytes=64)
         o_sc = keep.tile([P, S], U8, name="o_sc", align_bytes=64)
@@ -176,10 +192,12 @@ def tile_picked_elo8_none_po_kernel(
         out_words = out_1[0].rearrange("p n r -> p (n r)").bitcast(I32)
         rounded = [keep.tile([P, HALF * PACK], BF16, name="rounded%d" % h, align_bytes=64) for h in range(2)]
 
-        def round_columns(copy, h, result, r0, r1):
+        def hand_out(b, result, copy):
+            h, r0 = divmod(b * BLK, HALF)
+            nc.sync.dma_start(out=out_rows[:, :, b * BLK : (b + 1) * BLK], in_=result[:])
             copy(
-                out=rounded[h][:, r0 * PACK : r1 * PACK].rearrange("p (c i t) -> p c t i", i=4, t=PACK),
-                in_=result.rearrange("p t (c i) -> p c t i", i=4),
+                out=rounded[h][:, r0 * PACK : (r0 + BLK) * PACK].rearrange("p (c i t) -> p c t i", i=4, t=PACK),
+                in_=result[:].rearrange("p t (c i) -> p c t i", i=4),
             )
 
         def quantize_half(h):
@@ -187,39 +205,28 @@ def tile_picked_elo8_none_po_kernel(
             nc.vector.quantize_mx(out=o_codes[:, cols].bitcast(FP8X4), scales=o_sc[:, cols], in_=rounded[h][:])
             nc.sync.dma_start(out=out_words[:, cols], in_=o_codes[:, cols].bitcast(I32))
 
-        win = keep.tile([P, 2, PACK, HALF], F32, name="win")
-        for t in range(PACK):
-            nc.scalar.activation(out=win[:, :, t, :], in_=late_diffs[t][:], func=ACT.Sigmoid, scale=-1.0)
-        stages = [keep.tile([P, PACK, HALF], F32, name="stage%d" % i) for i in range(3)]
-        blocks = [slice(b * BLK, (b + 1) * BLK) for b in early_blocks]
-        terms = [(res_sum[:], 0.75), (win[:, 0, :, :], -0.75), (win[:, 1, :, :], -0.75)]
-        for i, (term, factor) in enumerate(terms):
-            before = stages[i - 1] if i else y_own[1]
-            for cols in blocks:
-                nc.vector.scalar_tensor_tensor(
-                    out=stages[i][:, :, cols],
-                    in0=term[:, :, cols],
-                    scalar=factor,
-                    in1=before[:, :, cols],
-                    op0=ALU.mult,
-                    op1=ALU.add,
-                )
-        late = stages[2]
-        nc.sync.dma_start(out=out_rows[:, :, HALF:S], in_=late[:])
-        for cols in blocks:
-            round_columns(nc.scalar.copy, 1, late[:, :, cols], cols.start, cols.stop)
-        results = []
-        for b, cols in enumerate(blocks):
-            result = keep.tile([P, PACK, BLK], F32, name="result%d" % b)
-            nc.vector.tensor_tensor(out=result[:], in0=moves[b][:], in1=y_own[0][:, :, cols], op=ALU.add)
-            nc.sync.dma_start(out=out_rows[:, :, cols], in_=result[:])
-            results.append(result)
-        round_columns(nc.scalar.copy, 0, results[0][:], 0, BLK)
-        quantize_half(1)
-        round_columns(nc.vector.tensor_copy, 0, results[1][:], BLK, HALF)
+        def finish_turned(b, own, copy):
+            result = keep.tile([P, PACK, BLK], F32, name="result", tag="diff%d_%d" % (len(CHUNKS) - 1, b + 1))
+            nc.vector.tensor_tensor(out=result[:], in0=moves[b][:], in1=own, op=ALU.add)
+            hand_out(b, result, copy)
+
+        def add_scaled(term, before, name):
+            after = keep.tile([P, PACK, BLK], F32, name=name)
+            nc.vector.scalar_tensor_tensor(out=after[:], in0=term, scalar=STEP, in1=before[:], op0=ALU.mult, op1=ALU.add)
+            return after
+
+        last = add_scaled(res_sum[:, :, BLK:HALF], y_own[2], "last0")
+        finish_turned(0, y_own[0][:, :, 0:BLK], nc.scalar.copy)
+        last = add_scaled(sig[2][:, 0, :, :], last, "last1")
+        finish_turned(1, y_own[0][:, :, BLK:HALF], nc.scalar.copy)
+        last = add_scaled(sig[2][:, 1, :, :], last, "last2")
+        hand_out(BLOCKS - 1, last, nc.scalar.copy)
         quantize_half(0)
-        for q in range(4):
+        finish_turned(2, y_own[1][:], nc.vector.tensor_copy)
+        quantize_half(1)
+        for q in range(QUADS):
             queue = nc.scalar if q % 2 else nc.sync
             queue.dma_start(
-                out=out_2[0, 4 * q : 4 * q + 4, :].bitcast(I32), in_=o_sc[32 * q : 32 * q + 4, :].bitcast(I32)
+                out=out_2[0, SCALE_ROWS * q : SCALE_ROWS * (q + 1), :].bitcast(I32),
+                in_=o_sc[32 * q : 32 * q + SCALE_ROWS, :].bitcast(I32),
             )

@@ -28,9 +28,6 @@ BLOCKS = S // BLK
 HALF = S // 2
 STEP = 0.75
 DEAL_SPLIT = 84
-CHUNKS = ((0, HALF), (HALF, HALF + BLK), (HALF + BLK, S))
-TURNED = 3
-SCALES_FIRST = 6
 
 
 def tile_picked_elo8_none_po_kernel(
@@ -45,8 +42,15 @@ def tile_picked_elo8_none_po_kernel(
         offs_t = lists.tile([P, S // GROUP], U16, name="offs_t")
         opp_t = [lists.tile([P, S // GROUP], U16, name="opp_t%d" % l) for l in range(GAMES)]
 
-        xs_raw = keep.tile([P, T], U8, name="xs_raw", align_bytes=64)
-        nc.vector.memset(xs_raw[:].bitcast(I32), 0)
+        xs_raw = keep.tile([P, PASSES * T], U8, name="xs_raw", align_bytes=64)
+        nc.gpsimd.memset(xs_raw[:, 0:T].bitcast(I32), 0)
+        nc.vector.memset(xs_raw[:, T:].bitcast(I32), 0)
+        xs = keep.tile([P, PASSES * S], U8, name="xs", align_bytes=64)
+        nc.vector.memset(xs[:].bitcast(I32), 0)
+        warm_in = keep.tile([P, 1], F32, name="warm_in")
+        warm_out = keep.tile([P, 1], F32, name="warm_out")
+        nc.vector.memset(warm_in[:], 0.0)
+        nc.scalar.activation(out=warm_out[:], in_=warm_in[:], func=ACT.Sigmoid)
         ident = keep.tile([P, P], F32, name="ident")
         make_identity(nc, ident[:])
 
@@ -55,39 +59,43 @@ def tile_picked_elo8_none_po_kernel(
         w_rows = w1.rearrange("(g p j) c -> g p j c", p=P, j=PACK)
         word_rows = [x_words[g].rearrange("p n r -> p (n r)").bitcast(I32) for g in range(PASSES)]
 
-        def load_scales(first, last):
-            for i in range(first, last):
-                g, q = divmod(i, QUADS)
-                row = 32 * q + SCALE_ROWS * g
-                nc.sync.dma_start(
-                    out=xs_raw[row : row + SCALE_ROWS, :].bitcast(I32),
-                    in_=x_scales[g, SCALE_ROWS * q : SCALE_ROWS * (q + 1), :].bitcast(I32),
-                )
-
+        spread = P // (QUADS * SCALE_ROWS)
+        xs_picked = keep.tile([P, PASSES * S], U8, name="xs_picked", align_bytes=64)
+        nc.sync.dma_start(out=w_raw[0][:, 0:2, :], in_=w_rows[0][:, 0:2, :])
         nc.sync.dma_start(out=offs_t[:], in_=offs)
-        nc.sync.dma_start(out=opp_t[0][:], in_=opp1)
-        nc.sync.dma_start(out=w_raw[0][:], in_=w_rows[0])
-        load_scales(0, SCALES_FIRST)
+        nc.sync.dma_start(
+            out=xs_raw[0:P:spread, :].bitcast(I32).rearrange("r (g c) -> r g c", g=PASSES),
+            in_=x_scales.bitcast(I32).rearrange("g r c -> r g c"),
+        )
+        nc.sync.dma_start(out=w_raw[0][:, 2:PACK, :], in_=w_rows[0][:, 2:PACK, :])
         nc.sync.dma_start(out=xw_raw[0][:].bitcast(I32), in_=word_rows[0])
-        load_scales(SCALES_FIRST, PASSES * QUADS)
         nc.sync.dma_start(out=w_raw[1][:], in_=w_rows[1])
+        for g in range(PASSES):
+            nc.vector.tensor_copy(
+                out=xs_picked[:, g * S : (g + 1) * S], in_=xs_raw[:, g * T : (g + 1) * T].indirect(offs_t[:])
+            )
+        for i in range(SCALE_ROWS):
+            nc.sync.dma_start(out=xs[i:P:32, :].bitcast(I32), in_=xs_picked[spread * i : P : 32, :].bitcast(I32))
         nc.sync.dma_start(out=xw_raw[1][:].bitcast(I32), in_=word_rows[1])
+        nc.sync.dma_start(out=opp_t[0][:], in_=opp1)
         nc.sync.dma_start(out=opp_t[1][:], in_=opp2)
         res_rows = [res.rearrange("(p t) n -> p t n", t=PACK) for res in (res1, res2)]
-        res_late = {}
-        for u in range(PACK // 2):
-            for l in range(GAMES):
-                res_late[l, u] = keep.tile([P, 2, HALF], F32, name="res_late%d_%d" % (l, u))
-                nc.sync.dma_start(out=res_late[l, u][:], in_=res_rows[l][:, 2 * u : 2 * u + 2, HALF:S])
+        CUT = 1
+        REST = PACK - CUT
+        late_rows = (slice(0, CUT), slice(CUT, PACK))
         res_early = [keep.tile([P, PACK, HALF], F32, name="res_early%d" % l) for l in range(GAMES)]
+        res_late = [[keep.tile([P, n, HALF], F32, name="res_late%d_%d" % (u, l), tag="res_late%d_%d" % (u, l)) for l in range(GAMES)] for u, n in enumerate((CUT, REST))]
+        for l in range(GAMES):
+            nc.sync.dma_start(out=res_late[1][l][:], in_=res_rows[l][:, late_rows[1], HALF:S])
         for l in range(GAMES):
             nc.sync.dma_start(out=res_early[l][:], in_=res_rows[l][:, :, 0:HALF])
+        for l in range(GAMES):
+            nc.sync.dma_start(out=res_late[0][l][:], in_=res_rows[l][:, late_rows[0], HALF:S])
 
         w_bf = [keep.tile([P, PACK * N], BF16, name="w_bf%d" % g, align_bytes=64) for g in range(PASSES)]
         w_codes = [keep.tile([P, N], U32, name="w_codes%d" % g, align_bytes=64) for g in range(PASSES)]
         w_sc = [keep.tile([P, N], U8, name="w_sc%d" % g, align_bytes=64) for g in range(PASSES)]
         xw = [keep.tile([P, S], U32, name="xw%d" % g, align_bytes=64) for g in range(PASSES)]
-        xs = keep.tile([P, S], U8, name="xs", align_bytes=64)
 
         def prepare_w(g):
             dealt = w_bf[g][:].rearrange("p (t m j) -> p m t j", t=PACK, j=PACK)
@@ -99,22 +107,23 @@ def tile_picked_elo8_none_po_kernel(
         prepare_w(0)
 
         parts = [(0, 0, HALF), (0, HALF, S)] + [(t, 0, S) for t in range(1, PACK)]
-        y_ps = [psum.tile([P, c1 - c0], F32, name="y_ps%d" % i, tag="bank%d" % i) for i, (t, c0, c1) in enumerate(parts)]
+        y_ps = {}
 
         def product(g, i):
             t, c0, c1 = parts[i]
+            if g == 0:
+                y_ps[i] = psum.tile([P, c1 - c0], F32, name="y_ps%d" % i, tag="bank%d" % i)
             nc.tensor.matmul_mx(
                 out=y_ps[i][:],
                 lhsT=w_codes[g][:, t * P : (t + 1) * P].bitcast(FP8X4),
                 lhsT_scale=w_sc[g][:, t * P : (t + 1) * P],
                 rhs=xw[g][:, c0:c1].bitcast(FP8X4),
-                rhs_scale=xs[SCALE_ROWS * g : P, c0:c1],
+                rhs_scale=xs[:, g * S + c0 : g * S + c1],
                 start=(g == 0),
                 stop=(g == PASSES - 1),
             )
 
         nc.vector.tensor_copy(out=xw[0][:], in_=xw_raw[0][:].indirect(offs_t[:]))
-        nc.vector.tensor_copy(out=xs[:], in_=xs_raw[:].indirect(offs_t[:]))
         for i in range(len(parts)):
             product(0, i)
         prepare_w(1)
@@ -124,67 +133,43 @@ def tile_picked_elo8_none_po_kernel(
                 in_=xw_raw[1][:].indirect(offs_t[:, h * HALF // GROUP : (h + 1) * HALF // GROUP]),
             )
 
-        res_sum = keep.tile([P, PACK, HALF], F32, name="res_sum")
-        for u in range(PACK // 2):
-            nc.vector.scalar_tensor_tensor(
-                out=res_sum[:, 2 * u : 2 * u + 2, :],
-                in0=res_late[0, u][:],
-                scalar=-float(GAMES),
-                in1=res_late[1, u][:],
-                op0=ALU.add,
-                op1=ALU.add,
-            )
+        res_sum = keep.tile([P, REST, HALF], F32, name="res_sum")
+        nc.vector.scalar_tensor_tensor(
+            out=res_sum[:], in0=res_late[1][0][:], scalar=-float(GAMES), in1=res_late[1][1][:], op0=ALU.add, op1=ALU.add
+        )
 
-        y_win = [keep.tile([P, S], F32, name="y_win%d" % t) for t in range(PACK)]
-        y_own = [keep.tile([P, PACK, c1 - c0], F32, name="y_own%d" % c) for c, (c0, c1) in enumerate(CHUNKS)]
+        z_win = [keep.tile([P, S], F32, name="z_win%d" % t, tag="z_win%d" % t) for t in range(PACK)]
+        z_own = [keep.tile([P, PACK, HALF], F32, name="z_own%d" % h) for h in range(2)]
         for i, (t, c0, c1) in enumerate(parts):
             product(1, i)
-            nc.scalar.copy(out=y_win[t][:, c0:c1], in_=y_ps[i][:])
+            nc.scalar.activation(out=z_win[t][:, c0:c1], in_=y_ps[i][:], func=ACT.Copy, scale=1.0 / STEP)
             if c0 == 0:
-                nc.scalar.copy(out=y_own[0][:, t, :], in_=y_ps[i][:, 0:HALF])
-        for c in range(1, len(CHUNKS)):
-            for t in range(PACK):
-                nc.sync.dma_start(out=y_own[c][:, t, :], in_=y_win[t][:, CHUNKS[c][0] : CHUNKS[c][1]])
+                nc.scalar.activation(out=z_own[0][:, t, :], in_=y_ps[i][:, 0:HALF], func=ACT.Copy, scale=1.0 / STEP)
+        for t in range(PACK):
+            nc.sync.dma_start(out=z_own[1][:, t, :], in_=z_win[t][:, HALF:S])
 
         def add_turned(bank, t, term, start, stop):
             nc.tensor.matmul(out=bank[:, t, :], lhsT=term, rhs=ident[:], start=start, stop=stop, is_transpose=True)
 
-        sums = [psum.tile([P, PACK, P], F32, name="sums", tag="bank%d" % (len(parts) + b)) for b in range(TURNED)]
-        early_blocks = HALF // BLK
-        for l in range(GAMES):
-            for b in range(early_blocks):
-                for t in range(PACK):
-                    add_turned(sums[b], t, res_early[l][:, t, b * BLK : (b + 1) * BLK], (l, t) == (0, 0), False)
-        for t in range(PACK):
-            add_turned(sums[early_blocks], t, res_sum[:, t, 0:BLK], t == 0, False)
+        units = [[(t, b) for t in range(PACK)] for b in range(2)] + [[(t, b) for t in range(CUT) for b in (2, 3)]]
+        sums = [psum.tile([P, len(units[n]), P], F32, name="sums", tag="bank%d" % (5 + n)) for n in range(len(units))]
 
-        sig = []
-        moves = []
-        for c, (c0, c1) in enumerate(CHUNKS):
-            sig.append(keep.tile([P, GAMES, PACK, c1 - c0], F32, name="sig%d" % c))
-            blocks = [b for b in range(c0 // BLK, c1 // BLK) if b < TURNED]
-            for t in range(PACK):
-                diff = keep.tile([P, GAMES, c1 - c0], F32, name="diff", tag="diff%d_%d" % (c, t))
-                for l in range(GAMES):
-                    nc.vector.tensor_tensor(
-                        out=diff[:, l, :],
-                        in0=y_win[t][:].indirect(opp_t[l][:, c0 // GROUP : c1 // GROUP]),
-                        in1=y_own[c][:, t, :],
-                        op=ALU.subtract,
-                    )
-                nc.scalar.activation(out=sig[c][:, :, t, :], in_=diff[:], func=ACT.Sigmoid)
-                for b in blocks:
-                    for l in range(GAMES):
-                        term = sig[c][:, l, t, b * BLK - c0 : (b + 1) * BLK - c0]
-                        add_turned(sums[b], t, term, False, (t, l) == (PACK - 1, GAMES - 1))
-            for b in blocks:
-                move_t = keep.tile([P, PACK, P], F32, name="move_t%d" % b)
-                bias = -STEP * GAMES if b < early_blocks else 0.0
-                nc.scalar.activation(out=move_t[:], in_=sums[b][:], func=ACT.Copy, scale=STEP, bias=bias)
-                move = psum.tile([P, PACK, BLK], F32, name="move", tag="bank%d" % b)
-                for t in range(PACK):
-                    nc.tensor.transpose(move[:, t, :], move_t[:, t, :], ident[:])
-                moves.append(move)
+        res_turned = (res_early, res_early, res_late[0])
+
+        def add_result(n, l):
+            for q, (t, b) in enumerate(units[n]):
+                c = b * BLK % HALF
+                add_turned(sums[n], q, res_turned[n][l][:, t, c : c + BLK], (l, q) == (0, 0), False)
+
+        def add_rating(n, q):
+            t, b = units[n][q]
+            add_turned(sums[n], q, z_win[t][:, b * BLK : (b + 1) * BLK], False, False)
+
+        def add_sigmoids(n, q):
+            t, b = units[n][q]
+            h, c = divmod(b * BLK, HALF)
+            for l in range(GAMES):
+                add_turned(sums[n], q, sig[h][:, t, l, c : c + BLK], False, (q, l) == (len(units[n]) - 1, GAMES - 1))
 
         o_codes = keep.tile([P, S], U32, name="o_codes", align_bytes=64)
         o_sc = keep.tile([P, S], U8, name="o_sc", align_bytes=64)
@@ -192,12 +177,11 @@ def tile_picked_elo8_none_po_kernel(
         out_words = out_1[0].rearrange("p n r -> p (n r)").bitcast(I32)
         rounded = [keep.tile([P, HALF * PACK], BF16, name="rounded%d" % h, align_bytes=64) for h in range(2)]
 
-        def hand_out(b, result, copy):
+        def round_block(b, result, copy):
             h, r0 = divmod(b * BLK, HALF)
-            nc.sync.dma_start(out=out_rows[:, :, b * BLK : (b + 1) * BLK], in_=result[:])
             copy(
                 out=rounded[h][:, r0 * PACK : (r0 + BLK) * PACK].rearrange("p (c i t) -> p c t i", i=4, t=PACK),
-                in_=result[:].rearrange("p t (c i) -> p c t i", i=4),
+                in_=result.rearrange("p t (c i) -> p c t i", i=4),
             )
 
         def quantize_half(h):
@@ -205,24 +189,100 @@ def tile_picked_elo8_none_po_kernel(
             nc.vector.quantize_mx(out=o_codes[:, cols].bitcast(FP8X4), scales=o_sc[:, cols], in_=rounded[h][:])
             nc.sync.dma_start(out=out_words[:, cols], in_=o_codes[:, cols].bitcast(I32))
 
-        def finish_turned(b, own, copy):
-            result = keep.tile([P, PACK, BLK], F32, name="result", tag="diff%d_%d" % (len(CHUNKS) - 1, b + 1))
-            nc.vector.tensor_tensor(out=result[:], in0=moves[b][:], in1=own, op=ALU.add)
-            hand_out(b, result, copy)
+        early = keep.tile([P, PACK, HALF], F32, name="early")
+        late = keep.tile([P, PACK, HALF], F32, name="late")
 
-        def add_scaled(term, before, name):
-            after = keep.tile([P, PACK, BLK], F32, name=name)
-            nc.vector.scalar_tensor_tensor(out=after[:], in0=term, scalar=STEP, in1=before[:], op0=ALU.mult, op1=ALU.add)
-            return after
+        sig = [keep.tile([P, PACK, GAMES, HALF], F32, name="sig%d" % h) for h in range(2)]
 
-        last = add_scaled(res_sum[:, :, BLK:HALF], y_own[2], "last0")
-        finish_turned(0, y_own[0][:, :, 0:BLK], nc.scalar.copy)
-        last = add_scaled(sig[2][:, 0, :, :], last, "last1")
-        finish_turned(1, y_own[0][:, :, BLK:HALF], nc.scalar.copy)
-        last = add_scaled(sig[2][:, 1, :, :], last, "last2")
-        hand_out(BLOCKS - 1, last, nc.scalar.copy)
+        move_t = [keep.tile([P, len(units[n]), P], F32, name="move_t%d" % n) for n in range(len(units))]
+
+        def constant(place, value):
+            nc.gpsimd.memset(place, value)
+            return place
+
+        step_a = constant(sig[1][:, 1, 0, 0:1], STEP)
+        one_b = constant(sig[1][:, 2, 0, 0:1], 1.0)
+        zero_b = constant(sig[1][:, 3, 0, 0:1], 0.0)
+        step_c = constant(move_t[2][:, 0, 0:1], STEP)
+        zero_c = constant(early[:, 0, BLK : BLK + 1], 0.0)
+
+        diffs = [keep.tile([P, PACK, GAMES, HALF], F32, name="diffs", tag=tag) for tag in ("res_late1_0", "diffs_late")]
+
+        def sigmoids(h, t, scale=STEP, bias=0.0):
+            diff = diffs[h][:, t, :, :]
+            for l in range(GAMES):
+                nc.vector.tensor_tensor(
+                    out=diff[:, l, :],
+                    in0=z_win[t][:].indirect(opp_t[l][:, h * HALF // GROUP : (h + 1) * HALF // GROUP]),
+                    in1=z_own[h][:, t, :],
+                    op=ALU.subtract,
+                )
+            nc.scalar.activation(out=sig[h][:, t, :, :], in_=diff, func=ACT.Sigmoid, scale=scale, bias=bias)
+
+        def leave(n, scale):
+            nc.scalar.activation(out=move_t[n][:], in_=sums[n][:], func=ACT.Copy, scale=scale, bias=-STEP * GAMES)
+            return move_t[n]
+
+        def turn_back(n, turned):
+            move = psum.tile([P, len(units[n]), BLK], F32, name="move", tag="bank%d" % n)
+            for q in range(len(units[n])):
+                nc.tensor.transpose(move[:, q, :], turned[:, q, :], ident[:])
+            return move
+
+        for l in range(GAMES):
+            for n in range(2):
+                add_result(n, l)
+        for q in range(PACK):
+            for n in range(2):
+                add_rating(n, q)
+        for t in range(PACK - 1):
+            sigmoids(0, t)
+        base = keep.tile([P, REST, HALF], F32, name="base")
+        nc.scalar.activation(out=base[:], in_=res_sum[:], func=ACT.Copy, scale=STEP)
+        sigmoids(0, PACK - 1)
+        add_sigmoids(0, 0)
+        add_sigmoids(1, 0)
+        for n in range(2):
+            for q in range(1, PACK):
+                add_sigmoids(n, q)
+        sigmoids(1, 0)
+        move_t0 = leave(0, step_a)
+        move0 = turn_back(0, move_t0)
+        for l in range(GAMES):
+            add_result(2, l)
+        for q in range(len(units[2])):
+            add_rating(2, q)
+        for q in range(len(units[2])):
+            add_sigmoids(2, q)
+        move_t1 = leave(1, STEP)
+        move1 = turn_back(1, move_t1)
+        sigmoids(1, 1)
+        nc.scalar.activation(out=early[:, :, 0:BLK], in_=move0[:], func=ACT.Identity, scale=one_b, bias=zero_b)
+        nc.sync.dma_start(out=out_rows[:, :, 0:BLK], in_=early[:, :, 0:BLK])
+        sigmoids(1, 2)
+        sigmoids(1, 3, step_c, zero_c)
+        move2 = turn_back(2, leave(2, STEP))
+        nc.scalar.copy(out=early[:, :, BLK:HALF], in_=move1[:])
+        nc.sync.dma_start(out=out_rows[:, :, BLK:HALF], in_=early[:, :, BLK:HALF])
+        round_block(0, early[:, :, 0:BLK], nc.scalar.copy)
+        nc.scalar.copy(out=late[:, 0:CUT, :].rearrange("p t c -> p (t c)"), in_=move2[:].rearrange("p q c -> p (q c)"))
+
+        def add_scaled(out, term, before):
+            nc.vector.scalar_tensor_tensor(out=out, in0=term, scalar=STEP, in1=before, op0=ALU.mult, op1=ALU.add)
+
+        with_z = keep.tile([P, REST, HALF], F32, name="with_z", tag="z_win%d" % (PACK - 1))
+        add_scaled(with_z[:], z_own[1][:, CUT:PACK, :], base[:])
+        with_one = keep.tile([P, REST, HALF], F32, name="with_one")
+        for before, after, l in ((with_z, with_one, 0), (with_one, late[:, CUT:PACK, :], 1)):
+            for h in range(2):
+                cols = slice(h * BLK, (h + 1) * BLK)
+                add_scaled(after[:, :, cols], sig[1][:, CUT:PACK, l, cols], before[:, :, cols])
+        for h in range(2):
+            nc.sync.dma_start(out=out_rows[:, :, HALF + h * BLK : HALF + (h + 1) * BLK], in_=late[:, :, h * BLK : (h + 1) * BLK])
+        round_block(1, early[:, :, BLK:HALF], nc.vector.tensor_copy)
+        round_block(2, late[:, :, 0:BLK], nc.scalar.copy)
+        round_block(3, late[:, :, BLK:HALF], nc.vector.tensor_copy)
         quantize_half(0)
-        finish_turned(2, y_own[1][:], nc.vector.tensor_copy)
         quantize_half(1)
         for q in range(QUADS):
             queue = nc.scalar if q % 2 else nc.sync

@@ -84,7 +84,7 @@ def tile_picked_elo8_none_po_kernel(
         REST = PACK - CUT
         late_rows = (slice(0, CUT), slice(CUT, PACK))
         res_early = [keep.tile([P, PACK, HALF], F32, name="res_early%d" % l) for l in range(GAMES)]
-        res_late = [[keep.tile([P, n, HALF], F32, name="res_late%d_%d" % (u, l), tag="res_late%d_%d" % (u, l)) for l in range(GAMES)] for u, n in enumerate((CUT, REST))]
+        res_late = [[keep.tile([P, n, HALF], F32, name="res_late%d_%d" % (u, l)) for l in range(GAMES)] for u, n in enumerate((CUT, REST))]
         for l in range(GAMES):
             nc.sync.dma_start(out=res_late[1][l][:], in_=res_rows[l][:, late_rows[1], HALF:S])
         for l in range(GAMES):
@@ -134,9 +134,17 @@ def tile_picked_elo8_none_po_kernel(
             )
 
         res_sum = keep.tile([P, REST, HALF], F32, name="res_sum")
-        nc.vector.scalar_tensor_tensor(
-            out=res_sum[:], in0=res_late[1][0][:], scalar=-float(GAMES), in1=res_late[1][1][:], op0=ALU.add, op1=ALU.add
-        )
+        minus_games = keep.tile([P, 1], F32, name="minus_games", tag="diffs_early")
+        nc.gpsimd.memset(minus_games[:], -float(GAMES))
+        for rows, scalar in ((slice(0, 1), minus_games[:]), (slice(1, REST), -float(GAMES))):
+            nc.vector.scalar_tensor_tensor(
+                out=res_sum[:, rows, :],
+                in0=res_late[1][0][:, rows, :],
+                scalar=scalar,
+                in1=res_late[1][1][:, rows, :],
+                op0=ALU.add,
+                op1=ALU.add,
+            )
 
         z_win = [keep.tile([P, S], F32, name="z_win%d" % t, tag="z_win%d" % t) for t in range(PACK)]
         z_own = [keep.tile([P, PACK, HALF], F32, name="z_own%d" % h) for h in range(2)]
@@ -152,47 +160,49 @@ def tile_picked_elo8_none_po_kernel(
             nc.tensor.matmul(out=bank[:, t, :], lhsT=term, rhs=ident[:], start=start, stop=stop, is_transpose=True)
 
         units = [[(t, b) for t in range(PACK)] for b in range(2)] + [[(t, b) for t in range(CUT) for b in (2, 3)]]
-        sums = [psum.tile([P, len(units[n]), P], F32, name="sums", tag="bank%d" % (5 + n)) for n in range(len(units))]
+        sums = [psum.tile([P, len(units[n]), P], F32, name="sums", tag="bank%d" % (5 + n)) for n in range(2)]
 
         res_turned = (res_early, res_early, res_late[0])
 
         def add_result(n, l):
             for q, (t, b) in enumerate(units[n]):
                 c = b * BLK % HALF
-                add_turned(sums[n], q, res_turned[n][l][:, t, c : c + BLK], (l, q) == (0, 0), False)
+                add_turned(sums[n], q, res_turned[n][l][:, t, c : c + BLK], False, False)
 
         def add_rating(n, q):
             t, b = units[n][q]
-            add_turned(sums[n], q, z_win[t][:, b * BLK : (b + 1) * BLK], False, False)
+            add_turned(sums[n], q, z_win[t][:, b * BLK : (b + 1) * BLK], q == 0, False)
 
         def add_sigmoids(n, q):
             t, b = units[n][q]
-            h, c = divmod(b * BLK, HALF)
             for l in range(GAMES):
-                add_turned(sums[n], q, sig[h][:, t, l, c : c + BLK], False, (q, l) == (len(units[n]) - 1, GAMES - 1))
+                add_turned(sums[n], q, sig_place(b // 2, t)[:, l, b % 2, :], False, (q, l) == (len(units[n]) - 1, GAMES - 1))
 
         o_codes = keep.tile([P, S], U32, name="o_codes", align_bytes=64)
         o_sc = keep.tile([P, S], U8, name="o_sc", align_bytes=64)
         out_rows = out_0.rearrange("(p t) n -> p t n", t=PACK)
         out_words = out_1[0].rearrange("p n r -> p (n r)").bitcast(I32)
-        rounded = [keep.tile([P, HALF * PACK], BF16, name="rounded%d" % h, align_bytes=64) for h in range(2)]
+        rounded = keep.tile([P, S * PACK], BF16, name="rounded", align_bytes=64)
 
-        def round_block(b, result, copy):
-            h, r0 = divmod(b * BLK, HALF)
+        def round_columns(c0, c1, copy):
+            source = early[:, :, c0:c1] if c1 <= HALF else late[:, :, c0 - HALF : c1 - HALF]
             copy(
-                out=rounded[h][:, r0 * PACK : (r0 + BLK) * PACK].rearrange("p (c i t) -> p c t i", i=4, t=PACK),
-                in_=result.rearrange("p t (c i) -> p c t i", i=4),
+                out=rounded[:, c0 * PACK : c1 * PACK].rearrange("p (c i t) -> p c t i", i=4, t=PACK),
+                in_=source.rearrange("p t (c i) -> p c t i", i=4),
             )
 
-        def quantize_half(h):
-            cols = slice(h * HALF, (h + 1) * HALF)
-            nc.vector.quantize_mx(out=o_codes[:, cols].bitcast(FP8X4), scales=o_sc[:, cols], in_=rounded[h][:])
-            nc.sync.dma_start(out=out_words[:, cols], in_=o_codes[:, cols].bitcast(I32))
+        def quantize(c0, c1):
+            nc.vector.quantize_mx(
+                out=o_codes[:, c0:c1].bitcast(FP8X4), scales=o_sc[:, c0:c1], in_=rounded[:, c0 * PACK : c1 * PACK]
+            )
+
+        def store_codes(c0, c1):
+            nc.sync.dma_start(out=out_words[:, c0:c1], in_=o_codes[:, c0:c1].bitcast(I32))
 
         early = keep.tile([P, PACK, HALF], F32, name="early")
         late = keep.tile([P, PACK, HALF], F32, name="late")
 
-        sig = [keep.tile([P, PACK, GAMES, HALF], F32, name="sig%d" % h) for h in range(2)]
+        sig = [keep.tile([P, n, GAMES, HALF], F32, name="sig%d" % h) for h, n in enumerate((PACK - 1, PACK))]
 
         move_t = [keep.tile([P, len(units[n]), P], F32, name="move_t%d" % n) for n in range(len(units))]
 
@@ -200,13 +210,17 @@ def tile_picked_elo8_none_po_kernel(
             nc.gpsimd.memset(place, value)
             return place
 
-        step_a = constant(sig[1][:, 1, 0, 0:1], STEP)
-        one_b = constant(sig[1][:, 2, 0, 0:1], 1.0)
-        zero_b = constant(sig[1][:, 3, 0, 0:1], 0.0)
-        step_c = constant(move_t[2][:, 0, 0:1], STEP)
-        zero_c = constant(early[:, 0, BLK : BLK + 1], 0.0)
+        step_held = constant(sig[1][:, 2, 0, 0:1], STEP)
+        zero_held = constant(sig[1][:, 3, 0, 0:1], 0.0)
+        late_flat = sig[1][:].rearrange("p t l c -> p (t l c)")
+        shared = late_flat[:, HALF : HALF + S].rearrange("p (b l c) -> p l b c", b=2, l=GAMES)
 
-        diffs = [keep.tile([P, PACK, GAMES, HALF], F32, name="diffs", tag=tag) for tag in ("res_late1_0", "diffs_late")]
+        def sig_place(h, t):
+            if (h, t) == (0, PACK - 1):
+                return shared
+            return sig[h][:, t, :, :].rearrange("p l (b c) -> p l b c", b=2)
+
+        diffs = [keep.tile([P, PACK, GAMES, HALF], F32, name="diffs", tag=tag) for tag in ("diffs_early", "diffs_late")]
 
         def sigmoids(h, t, scale=STEP, bias=0.0):
             diff = diffs[h][:, t, :, :]
@@ -217,7 +231,8 @@ def tile_picked_elo8_none_po_kernel(
                     in1=z_own[h][:, t, :],
                     op=ALU.subtract,
                 )
-            nc.scalar.activation(out=sig[h][:, t, :, :], in_=diff, func=ACT.Sigmoid, scale=scale, bias=bias)
+            source = diff.rearrange("p l (b c) -> p l b c", b=2)
+            nc.scalar.activation(out=sig_place(h, t), in_=source, func=ACT.Sigmoid, scale=scale, bias=bias)
 
         def leave(n, scale):
             nc.scalar.activation(out=move_t[n][:], in_=sums[n][:], func=ACT.Copy, scale=scale, bias=-STEP * GAMES)
@@ -230,11 +245,11 @@ def tile_picked_elo8_none_po_kernel(
             return move
 
         for l in range(GAMES):
+            for q in (2 * l, 2 * l + 1):
+                for n in range(2):
+                    add_rating(n, q)
             for n in range(2):
                 add_result(n, l)
-        for q in range(PACK):
-            for n in range(2):
-                add_rating(n, q)
         for t in range(PACK - 1):
             sigmoids(0, t)
         base = keep.tile([P, REST, HALF], F32, name="base")
@@ -245,32 +260,33 @@ def tile_picked_elo8_none_po_kernel(
         for n in range(2):
             for q in range(1, PACK):
                 add_sigmoids(n, q)
-        sigmoids(1, 0)
-        move_t0 = leave(0, step_a)
+        move_t0 = leave(0, STEP)
         move0 = turn_back(0, move_t0)
-        for l in range(GAMES):
-            add_result(2, l)
+        sigmoids(1, 0)
+        sums.append(psum.tile([P, len(units[2]), P], F32, name="sums", tag="bank5"))
         for q in range(len(units[2])):
             add_rating(2, q)
+        for l in range(GAMES):
+            add_result(2, l)
+        move1 = turn_back(1, leave(1, STEP))
         for q in range(len(units[2])):
             add_sigmoids(2, q)
-        move_t1 = leave(1, STEP)
-        move1 = turn_back(1, move_t1)
-        sigmoids(1, 1)
-        nc.scalar.activation(out=early[:, :, 0:BLK], in_=move0[:], func=ACT.Identity, scale=one_b, bias=zero_b)
+        sigmoids(1, 1, step_held, zero_held)
+        nc.scalar.copy(out=early[:, :, 0:BLK], in_=move0[:])
         nc.sync.dma_start(out=out_rows[:, :, 0:BLK], in_=early[:, :, 0:BLK])
         sigmoids(1, 2)
-        sigmoids(1, 3, step_c, zero_c)
+        sigmoids(1, 3)
+        round_columns(0, BLK, nc.scalar.copy)
         move2 = turn_back(2, leave(2, STEP))
         nc.scalar.copy(out=early[:, :, BLK:HALF], in_=move1[:])
         nc.sync.dma_start(out=out_rows[:, :, BLK:HALF], in_=early[:, :, BLK:HALF])
-        round_block(0, early[:, :, 0:BLK], nc.scalar.copy)
         nc.scalar.copy(out=late[:, 0:CUT, :].rearrange("p t c -> p (t c)"), in_=move2[:].rearrange("p q c -> p (q c)"))
+        round_columns(BLK, HALF, nc.scalar.copy)
 
         def add_scaled(out, term, before):
             nc.vector.scalar_tensor_tensor(out=out, in0=term, scalar=STEP, in1=before, op0=ALU.mult, op1=ALU.add)
 
-        with_z = keep.tile([P, REST, HALF], F32, name="with_z", tag="z_win%d" % (PACK - 1))
+        with_z = keep.tile([P, REST, HALF], F32, name="with_z", tag="z_win%d" % (PACK - 2))
         add_scaled(with_z[:], z_own[1][:, CUT:PACK, :], base[:])
         with_one = keep.tile([P, REST, HALF], F32, name="with_one")
         for before, after, l in ((with_z, with_one, 0), (with_one, late[:, CUT:PACK, :], 1)):
@@ -279,11 +295,13 @@ def tile_picked_elo8_none_po_kernel(
                 add_scaled(after[:, :, cols], sig[1][:, CUT:PACK, l, cols], before[:, :, cols])
         for h in range(2):
             nc.sync.dma_start(out=out_rows[:, :, HALF + h * BLK : HALF + (h + 1) * BLK], in_=late[:, :, h * BLK : (h + 1) * BLK])
-        round_block(1, early[:, :, BLK:HALF], nc.vector.tensor_copy)
-        round_block(2, late[:, :, 0:BLK], nc.scalar.copy)
-        round_block(3, late[:, :, BLK:HALF], nc.vector.tensor_copy)
-        quantize_half(0)
-        quantize_half(1)
+        round_columns(HALF, HALF + BLK, nc.scalar.copy)
+        quantize(0, HALF)
+        store_codes(0, HALF)
+        round_columns(HALF + BLK, S, nc.vector.tensor_copy)
+        quantize(HALF, HALF + BLK)
+        quantize(HALF + BLK, S)
+        store_codes(HALF, S)
         for q in range(QUADS):
             queue = nc.scalar if q % 2 else nc.sync
             queue.dma_start(

@@ -273,14 +273,14 @@ def tile_picked_elo8_none_po_kernel(
             add_sigmoids(2, q)
         sigmoids(1, 1, step_held, zero_held)
         nc.scalar.copy(out=early[:, :, 0:BLK], in_=move0[:])
-        nc.sync.dma_start(out=out_rows[:, :, 0:BLK], in_=early[:, :, 0:BLK])
         sigmoids(1, 2)
-        sigmoids(1, 3)
-        round_columns(0, BLK, nc.scalar.copy)
-        move2 = turn_back(2, leave(2, STEP))
         nc.scalar.copy(out=early[:, :, BLK:HALF], in_=move1[:])
-        nc.sync.dma_start(out=out_rows[:, :, BLK:HALF], in_=early[:, :, BLK:HALF])
+        nc.sync.dma_start(out=out_rows[:, :, 0:HALF], in_=early[:])
+        sigmoids(1, 3)
+        move2 = turn_back(2, leave(2, STEP))
+        round_columns(0, BLK, nc.scalar.copy)
         nc.scalar.copy(out=late[:, 0:CUT, :].rearrange("p t c -> p (t c)"), in_=move2[:].rearrange("p q c -> p (q c)"))
+        nc.sync.dma_start(out=out_rows[:, 0:CUT, HALF:S], in_=late[:, 0:CUT, :])
         round_columns(BLK, HALF, nc.scalar.copy)
 
         def add_scaled(out, term, before):
@@ -293,8 +293,7 @@ def tile_picked_elo8_none_po_kernel(
             for h in range(2):
                 cols = slice(h * BLK, (h + 1) * BLK)
                 add_scaled(after[:, :, cols], sig[1][:, CUT:PACK, l, cols], before[:, :, cols])
-        for h in range(2):
-            nc.sync.dma_start(out=out_rows[:, :, HALF + h * BLK : HALF + (h + 1) * BLK], in_=late[:, :, h * BLK : (h + 1) * BLK])
+        nc.sync.dma_start(out=out_rows[:, CUT:PACK, HALF:S], in_=late[:, CUT:PACK, :])
         round_columns(HALF, HALF + BLK, nc.scalar.copy)
         quantize(0, HALF)
         store_codes(0, HALF)

@@ -82,15 +82,19 @@ def tile_picked_elo8_none_po_kernel(
         res_rows = [res.rearrange("(p t) n -> p t n", t=PACK) for res in (res1, res2)]
         CUT = 1
         REST = PACK - CUT
-        late_rows = (slice(0, CUT), slice(CUT, PACK))
+        late_rows = (slice(0, CUT), slice(CUT, CUT + 1), slice(CUT + 1, PACK))
         res_early = [keep.tile([P, PACK, HALF], F32, name="res_early%d" % l) for l in range(GAMES)]
-        res_late = [[keep.tile([P, n, HALF], F32, name="res_late%d_%d" % (u, l)) for l in range(GAMES)] for u, n in enumerate((CUT, REST))]
-        for l in range(GAMES):
-            nc.sync.dma_start(out=res_late[1][l][:], in_=res_rows[l][:, late_rows[1], HALF:S])
+        res_late = [keep.tile([P, PACK, HALF], F32, name="res_late%d" % l) for l in range(GAMES)]
+
+        def load_late(rows):
+            for l in range(GAMES):
+                nc.sync.dma_start(out=res_late[l][:, rows, :], in_=res_rows[l][:, rows, HALF:S])
+
+        load_late(late_rows[2])
+        load_late(late_rows[1])
         for l in range(GAMES):
             nc.sync.dma_start(out=res_early[l][:], in_=res_rows[l][:, :, 0:HALF])
-        for l in range(GAMES):
-            nc.sync.dma_start(out=res_late[0][l][:], in_=res_rows[l][:, late_rows[0], HALF:S])
+        load_late(late_rows[0])
 
         w_bf = [keep.tile([P, PACK * N], BF16, name="w_bf%d" % g, align_bytes=64) for g in range(PASSES)]
         w_codes = [keep.tile([P, N], U32, name="w_codes%d" % g, align_bytes=64) for g in range(PASSES)]
@@ -136,12 +140,12 @@ def tile_picked_elo8_none_po_kernel(
         res_sum = keep.tile([P, REST, HALF], F32, name="res_sum")
         minus_games = keep.tile([P, 1], F32, name="minus_games", tag="diffs_early")
         nc.gpsimd.memset(minus_games[:], -float(GAMES))
-        for rows, scalar in ((slice(0, 1), minus_games[:]), (slice(1, REST), -float(GAMES))):
+        for rows, scalar in ((late_rows[2], -float(GAMES)), (late_rows[1], minus_games[:])):
             nc.vector.scalar_tensor_tensor(
-                out=res_sum[:, rows, :],
-                in0=res_late[1][0][:, rows, :],
+                out=res_sum[:, rows.start - CUT : rows.stop - CUT, :],
+                in0=res_late[0][:, rows, :],
                 scalar=scalar,
-                in1=res_late[1][1][:, rows, :],
+                in1=res_late[1][:, rows, :],
                 op0=ALU.add,
                 op1=ALU.add,
             )
@@ -162,7 +166,7 @@ def tile_picked_elo8_none_po_kernel(
         units = [[(t, b) for t in range(PACK)] for b in range(2)] + [[(t, b) for t in range(CUT) for b in (2, 3)]]
         sums = [psum.tile([P, len(units[n]), P], F32, name="sums", tag="bank%d" % (5 + n)) for n in range(2)]
 
-        res_turned = (res_early, res_early, res_late[0])
+        res_turned = (res_early, res_early, res_late)
 
         def add_result(n, l):
             for q, (t, b) in enumerate(units[n]):
@@ -222,7 +226,7 @@ def tile_picked_elo8_none_po_kernel(
 
         diffs = [keep.tile([P, PACK, GAMES, HALF], F32, name="diffs", tag=tag) for tag in ("diffs_early", "diffs_late")]
 
-        def sigmoids(h, t, scale=STEP, bias=0.0):
+        def sigmoids(h, t, scale=STEP, bias=0.0, pieces=(slice(0, GAMES),)):
             diff = diffs[h][:, t, :, :]
             for l in range(GAMES):
                 nc.vector.tensor_tensor(
@@ -232,7 +236,10 @@ def tile_picked_elo8_none_po_kernel(
                     op=ALU.subtract,
                 )
             source = diff.rearrange("p l (b c) -> p l b c", b=2)
-            nc.scalar.activation(out=sig_place(h, t), in_=source, func=ACT.Sigmoid, scale=scale, bias=bias)
+            for games in pieces:
+                nc.scalar.activation(
+                    out=sig_place(h, t)[:, games], in_=source[:, games], func=ACT.Sigmoid, scale=scale, bias=bias
+                )
 
         def leave(n, scale):
             nc.scalar.activation(out=move_t[n][:], in_=sums[n][:], func=ACT.Copy, scale=scale, bias=-STEP * GAMES)
@@ -276,7 +283,7 @@ def tile_picked_elo8_none_po_kernel(
         sigmoids(1, 2)
         nc.scalar.copy(out=early[:, :, BLK:HALF], in_=move1[:])
         nc.sync.dma_start(out=out_rows[:, :, 0:HALF], in_=early[:])
-        sigmoids(1, 3)
+        sigmoids(1, 3, pieces=(slice(0, 1), slice(1, 2)))
         move2 = turn_back(2, leave(2, STEP))
         round_columns(0, BLK, nc.scalar.copy)
         nc.scalar.copy(out=late[:, 0:CUT, :].rearrange("p t c -> p (t c)"), in_=move2[:].rearrange("p q c -> p (q c)"))
@@ -287,13 +294,16 @@ def tile_picked_elo8_none_po_kernel(
             nc.vector.scalar_tensor_tensor(out=out, in0=term, scalar=STEP, in1=before, op0=ALU.mult, op1=ALU.add)
 
         with_z = keep.tile([P, REST, HALF], F32, name="with_z", tag="z_win%d" % (PACK - 2))
-        add_scaled(with_z[:], z_own[1][:, CUT:PACK, :], base[:])
         with_one = keep.tile([P, REST, HALF], F32, name="with_one")
+        one_row, two_rows = slice(0, 1), slice(1, REST)
+        for rows in (one_row, two_rows):
+            add_scaled(with_z[:, rows, :], z_own[1][:, CUT:PACK, :][:, rows, :], base[:, rows, :])
+        pieces = ((one_row, slice(0, HALF)), (two_rows, slice(0, BLK)), (two_rows, slice(BLK, HALF)))
         for before, after, l in ((with_z, with_one, 0), (with_one, late[:, CUT:PACK, :], 1)):
-            for h in range(2):
-                cols = slice(h * BLK, (h + 1) * BLK)
-                add_scaled(after[:, :, cols], sig[1][:, CUT:PACK, l, cols], before[:, :, cols])
-        nc.sync.dma_start(out=out_rows[:, CUT:PACK, HALF:S], in_=late[:, CUT:PACK, :])
+            for rows, cols in pieces:
+                add_scaled(after[:, rows, cols], sig[1][:, CUT:PACK, l, :][:, rows, cols], before[:, rows, cols])
+        for rows in late_rows[1:]:
+            nc.sync.dma_start(out=out_rows[:, rows, HALF:S], in_=late[:, rows, :])
         round_columns(HALF, HALF + BLK, nc.scalar.copy)
         quantize(0, HALF)
         store_codes(0, HALF)

@@ -283,11 +283,10 @@ def tile_picked_elo8_none_po_kernel(
         sigmoids(1, 2)
         nc.scalar.copy(out=early[:, :, BLK:HALF], in_=move1[:])
         nc.sync.dma_start(out=out_rows[:, :, 0:HALF], in_=early[:])
-        sigmoids(1, 3, pieces=(slice(0, 1), slice(1, 2)))
         move2 = turn_back(2, leave(2, STEP))
-        round_columns(0, BLK, nc.scalar.copy)
+        sigmoids(1, 3, pieces=(slice(0, 1), slice(1, 2)))
         nc.scalar.copy(out=late[:, 0:CUT, :].rearrange("p t c -> p (t c)"), in_=move2[:].rearrange("p q c -> p (q c)"))
-        nc.sync.dma_start(out=out_rows[:, 0:CUT, HALF:S], in_=late[:, 0:CUT, :])
+        round_columns(0, BLK, nc.scalar.copy)
         round_columns(BLK, HALF, nc.scalar.copy)
 
         def add_scaled(out, term, before):
@@ -302,7 +301,7 @@ def tile_picked_elo8_none_po_kernel(
         for before, after, l in ((with_z, with_one, 0), (with_one, late[:, CUT:PACK, :], 1)):
             for rows, cols in pieces:
                 add_scaled(after[:, rows, cols], sig[1][:, CUT:PACK, l, :][:, rows, cols], before[:, rows, cols])
-        for rows in late_rows[1:]:
+        for rows in (slice(0, 2), slice(2, PACK)):
             nc.sync.dma_start(out=out_rows[:, rows, HALF:S], in_=late[:, rows, :])
         round_columns(HALF, HALF + BLK, nc.scalar.copy)
         quantize(0, HALF)

@@ -47,10 +47,6 @@ def tile_picked_elo8_none_po_kernel(
         nc.vector.memset(xs_raw[:, T:].bitcast(I32), 0)
         xs = keep.tile([P, PASSES * S], U8, name="xs", align_bytes=64)
         nc.vector.memset(xs[:].bitcast(I32), 0)
-        warm_in = keep.tile([P, 1], F32, name="warm_in")
-        warm_out = keep.tile([P, 1], F32, name="warm_out")
-        nc.vector.memset(warm_in[:], 0.0)
-        nc.scalar.activation(out=warm_out[:], in_=warm_in[:], func=ACT.Sigmoid)
         ident = keep.tile([P, P], F32, name="ident")
         make_identity(nc, ident[:])
 

@@ -49,6 +49,8 @@ def tile_picked_elo8_none_po_kernel(
         nc.vector.memset(xs[:].bitcast(I32), 0)
         ident = keep.tile([P, P], F32, name="ident")
         make_identity(nc, ident[:])
+        warm = keep.tile([P, 1], F32, name="warm")
+        nc.scalar.activation(out=warm[:], in_=ident[:, 0:1], func=ACT.Sigmoid)
 
         xw_raw = [keep.tile([P, T], U32, name="xw_raw%d" % g, align_bytes=64) for g in range(PASSES)]
         w_raw = [keep.tile([P, PACK, N], F32, name="w_raw%d" % g) for g in range(PASSES)]
@@ -73,24 +75,13 @@ def tile_picked_elo8_none_po_kernel(
         for i in range(SCALE_ROWS):
             nc.sync.dma_start(out=xs[i:P:32, :].bitcast(I32), in_=xs_picked[spread * i : P : 32, :].bitcast(I32))
         nc.sync.dma_start(out=xw_raw[1][:].bitcast(I32), in_=word_rows[1])
+        res_rows = [res.rearrange("(p t) n -> p t n", t=PACK) for res in (res1, res2)]
+        res_half = [[keep.tile([P, PACK, HALF], F32, name="res%d_%d" % (l, h)) for h in range(2)] for l in range(GAMES)]
         nc.sync.dma_start(out=opp_t[0][:], in_=opp1)
         nc.sync.dma_start(out=opp_t[1][:], in_=opp2)
-        res_rows = [res.rearrange("(p t) n -> p t n", t=PACK) for res in (res1, res2)]
-        CUT = 1
-        REST = PACK - CUT
-        late_rows = (slice(0, CUT), slice(CUT, CUT + 1), slice(CUT + 1, PACK))
-        res_early = [keep.tile([P, PACK, HALF], F32, name="res_early%d" % l) for l in range(GAMES)]
-        res_late = [keep.tile([P, PACK, HALF], F32, name="res_late%d" % l) for l in range(GAMES)]
-
-        def load_late(rows):
+        for h, t0, t1 in ((1, 1, 2), (1, 2, PACK), (0, 0, 2), (0, 2, PACK), (1, 0, 1)):
             for l in range(GAMES):
-                nc.sync.dma_start(out=res_late[l][:, rows, :], in_=res_rows[l][:, rows, HALF:S])
-
-        load_late(late_rows[2])
-        load_late(late_rows[1])
-        for l in range(GAMES):
-            nc.sync.dma_start(out=res_early[l][:], in_=res_rows[l][:, :, 0:HALF])
-        load_late(late_rows[0])
+                nc.sync.dma_start(out=res_half[l][h][:, t0:t1, :], in_=res_rows[l][:, t0:t1, h * HALF : (h + 1) * HALF])
 
         w_bf = [keep.tile([P, PACK * N], BF16, name="w_bf%d" % g, align_bytes=64) for g in range(PASSES)]
         w_codes = [keep.tile([P, N], U32, name="w_codes%d" % g, align_bytes=64) for g in range(PASSES)]
@@ -106,13 +97,15 @@ def tile_picked_elo8_none_po_kernel(
 
         prepare_w(0)
 
-        parts = [(0, 0, HALF), (0, HALF, S)] + [(t, 0, S) for t in range(1, PACK)]
+        pieces_x = ((0, HALF), (HALF, S))
+        parts = [(0, c0, c1) for c0, c1 in pieces_x] + [(t, 0, S) for t in range(1, PACK)]
+        part_banks = (0, 1, 2, 3, 4)
         y_ps = {}
 
         def product(g, i):
             t, c0, c1 = parts[i]
             if g == 0:
-                y_ps[i] = psum.tile([P, c1 - c0], F32, name="y_ps%d" % i, tag="bank%d" % i)
+                y_ps[i] = psum.tile([P, c1 - c0], F32, name="y_ps%d" % i, tag="bank%d" % part_banks[i])
             nc.tensor.matmul_mx(
                 out=y_ps[i][:],
                 lhsT=w_codes[g][:, t * P : (t + 1) * P].bitcast(FP8X4),
@@ -127,68 +120,126 @@ def tile_picked_elo8_none_po_kernel(
         for i in range(len(parts)):
             product(0, i)
         prepare_w(1)
-        for h in range(2):
-            nc.vector.tensor_copy(
-                out=xw[1][:, h * HALF : (h + 1) * HALF],
-                in_=xw_raw[1][:].indirect(offs_t[:, h * HALF // GROUP : (h + 1) * HALF // GROUP]),
-            )
+        for c0, c1 in ((0, HALF), (HALF, S)):
+            nc.vector.tensor_copy(out=xw[1][:, c0:c1], in_=xw_raw[1][:].indirect(offs_t[:, c0 // GROUP : c1 // GROUP]))
 
-        res_sum = keep.tile([P, REST, HALF], F32, name="res_sum")
+        res_sum = keep.tile([P, PACK - 1, HALF], F32, name="res_sum")
         minus_games = keep.tile([P, 1], F32, name="minus_games", tag="diffs_early")
         nc.gpsimd.memset(minus_games[:], -float(GAMES))
-        for rows, scalar in ((late_rows[2], -float(GAMES)), (late_rows[1], minus_games[:])):
+        sums_of_results = (
+            (0, slice(0, BLK), 0.0),
+            (0, slice(BLK, HALF), -float(GAMES)),
+            (1, slice(0, HALF), minus_games[:]),
+            (2, slice(0, HALF), -float(GAMES)),
+        )
+        for r, cols, scalar in sums_of_results:
             nc.vector.scalar_tensor_tensor(
-                out=res_sum[:, rows.start - CUT : rows.stop - CUT, :],
-                in0=res_late[0][:, rows, :],
+                out=res_sum[:, r, cols],
+                in0=res_half[0][1][:, 1 + r, cols],
                 scalar=scalar,
-                in1=res_late[1][:, rows, :],
+                in1=res_half[1][1][:, 1 + r, cols],
                 op0=ALU.add,
                 op1=ALU.add,
             )
 
         z_win = [keep.tile([P, S], F32, name="z_win%d" % t, tag="z_win%d" % t) for t in range(PACK)]
         z_own = [keep.tile([P, PACK, HALF], F32, name="z_own%d" % h) for h in range(2)]
-        for i, (t, c0, c1) in enumerate(parts):
-            product(1, i)
-            nc.scalar.activation(out=z_win[t][:, c0:c1], in_=y_ps[i][:], func=ACT.Copy, scale=1.0 / STEP)
-            if c0 == 0:
-                nc.scalar.activation(out=z_own[0][:, t, :], in_=y_ps[i][:, 0:HALF], func=ACT.Copy, scale=1.0 / STEP)
-        for t in range(PACK):
+
+        def window(t):
+            for i, (row, c0, c1) in enumerate(parts):
+                if row == t:
+                    nc.scalar.activation(out=z_win[t][:, c0:c1], in_=y_ps[i][:], func=ACT.Copy, scale=1.0 / STEP)
+                    if c0 == 0:
+                        nc.scalar.activation(out=z_own[0][:, t, :], in_=y_ps[i][:, 0:HALF], func=ACT.Copy, scale=1.0 / STEP)
             nc.sync.dma_start(out=z_own[1][:, t, :], in_=z_win[t][:, HALF:S])
 
-        def add_turned(bank, t, term, start, stop):
-            nc.tensor.matmul(out=bank[:, t, :], lhsT=term, rhs=ident[:], start=start, stop=stop, is_transpose=True)
+        for i in range(len(parts)):
+            product(1, i)
 
-        units = [[(t, b) for t in range(PACK)] for b in range(2)] + [[(t, b) for t in range(CUT) for b in (2, 3)]]
-        sums = [psum.tile([P, len(units[n]), P], F32, name="sums", tag="bank%d" % (5 + n)) for n in range(2)]
+        groups = ((0, 0), (2, 0), (0, 1))
+        sums = [psum.tile([P, 2, 2, P], F32, name="sums", tag="bank%d" % bank) for bank in (5, 6)]
 
-        res_turned = (res_early, res_early, res_late)
+        def blocks(n, r):
+            return range(1 if (n, r) == (2, 1) else 2)
 
-        def add_result(n, l):
-            for q, (t, b) in enumerate(units[n]):
-                c = b * BLK % HALF
-                add_turned(sums[n], q, res_turned[n][l][:, t, c : c + BLK], False, False)
+        def add_rows(n, t, term, start=False, stop=False):
+            for b in blocks(n, t - groups[n][0]):
+                nc.tensor.matmul(
+                    out=sums[n][:, t - groups[n][0], b, :],
+                    lhsT=term[:, b * BLK : (b + 1) * BLK],
+                    rhs=ident[:],
+                    start=start and b == 0,
+                    stop=stop and b == blocks(n, t - groups[n][0])[-1],
+                    is_transpose=True,
+                )
 
-        def add_rating(n, q):
-            t, b = units[n][q]
-            add_turned(sums[n], q, z_win[t][:, b * BLK : (b + 1) * BLK], q == 0, False)
+        def rating(t, h):
+            return z_win[t][:, h * HALF : (h + 1) * HALF]
 
-        def add_sigmoids(n, q):
-            t, b = units[n][q]
+        def result(l, t, h):
+            return res_half[l][h][:, t, :]
+
+        diffs = [keep.tile([P, PACK, GAMES, HALF], F32, name="diffs", tag=tag) for tag in ("diffs_early", "diffs_late")]
+
+        def differences(h, t):
             for l in range(GAMES):
-                add_turned(sums[n], q, sig_place(b // 2, t)[:, l, b % 2, :], False, (q, l) == (len(units[n]) - 1, GAMES - 1))
+                nc.vector.tensor_tensor(
+                    out=diffs[h][:, t, l, :],
+                    in0=z_win[t][:].indirect(opp_t[l][:, h * HALF // GROUP : (h + 1) * HALF // GROUP]),
+                    in1=z_own[h][:, t, :],
+                    op=ALU.subtract,
+                )
+
+        def sigmoids(h, t, out, pieces=(slice(0, GAMES),)):
+            differences(h, t)
+            for games in pieces:
+                nc.scalar.activation(out=out[:, games, :], in_=diffs[h][:, t, games, :], func=ACT.Sigmoid, scale=STEP)
+            return out
+
+        def sig_tile(tag):
+            return keep.tile([P, GAMES, HALF], F32, name="sig", tag=tag)[:]
+
+        def add_sigmoids(n, t, sig, stop=False):
+            for l in range(GAMES):
+                add_rows(n, t, sig[:, l, :], stop=stop and l == GAMES - 1)
+
+        def used(n, tile):
+            return tile[:].rearrange("p r b c -> p (r b c)")[:, 0 : (3 if n == 2 else 4) * BLK]
+
+        def leave(n):
+            turned = keep.tile([P, 2, 2, P], F32, name="turned", tag="turned%d" % n)
+            nc.scalar.activation(out=used(n, turned), in_=used(n, sums[n]), func=ACT.Copy, scale=STEP, bias=-STEP * GAMES)
+            return turned
+
+        def turn_back(n, turned):
+            back = psum.tile([P, 2, 2, BLK], F32, name="back", tag="bank%d" % (0, 1, 7)[n])
+            for r in range(2):
+                for b in blocks(n, r):
+                    nc.tensor.transpose(back[:, r, b, :], turned[:, r, b, :], ident[:])
+            return back
+
+        halves = [keep.tile([P, PACK, HALF], F32, name="half%d" % h) for h in range(2)]
+        out_rows = out_0.rearrange("(p t) n -> p t n", t=PACK)
+
+        def store_rows(t0, h):
+            nc.sync.dma_start(out=out_rows[:, t0 : t0 + 2, h * HALF : (h + 1) * HALF], in_=halves[h][:, t0 : t0 + 2, :])
+
+        def finish(n, back):
+            t0, h = groups[n]
+            place = halves[h][:, t0 : t0 + 2, :].rearrange("p r c -> p (r c)")
+            nc.scalar.copy(out=place[:, 0 : (3 if n == 2 else 4) * BLK], in_=used(n, back))
+            if n < 2:
+                store_rows(t0, h)
 
         o_codes = keep.tile([P, S], U32, name="o_codes", align_bytes=64)
         o_sc = keep.tile([P, S], U8, name="o_sc", align_bytes=64)
-        out_rows = out_0.rearrange("(p t) n -> p t n", t=PACK)
         out_words = out_1[0].rearrange("p n r -> p (n r)").bitcast(I32)
         rounded = keep.tile([P, S * PACK], BF16, name="rounded", align_bytes=64)
 
         def round_columns(c0, c1, copy):
-            source = early[:, :, c0:c1] if c1 <= HALF else late[:, :, c0 - HALF : c1 - HALF]
             copy(
                 out=rounded[:, c0 * PACK : c1 * PACK].rearrange("p (c i t) -> p c t i", i=4, t=PACK),
-                in_=source.rearrange("p t (c i) -> p c t i", i=4),
+                in_=halves[c0 // HALF][:, :, c0 % HALF : (c1 - 1) % HALF + 1].rearrange("p t (c i) -> p c t i", i=4),
             )
 
         def quantize(c0, c1):
@@ -199,110 +250,71 @@ def tile_picked_elo8_none_po_kernel(
         def store_codes(c0, c1):
             nc.sync.dma_start(out=out_words[:, c0:c1], in_=o_codes[:, c0:c1].bitcast(I32))
 
-        early = keep.tile([P, PACK, HALF], F32, name="early")
-        late = keep.tile([P, PACK, HALF], F32, name="late")
-
-        sig = [keep.tile([P, n, GAMES, HALF], F32, name="sig%d" % h) for h, n in enumerate((PACK - 1, PACK))]
-
-        move_t = [keep.tile([P, len(units[n]), P], F32, name="move_t%d" % n) for n in range(len(units))]
-
-        def constant(place, value):
-            nc.gpsimd.memset(place, value)
-            return place
-
-        step_held = constant(sig[1][:, 2, 0, 0:1], STEP)
-        zero_held = constant(sig[1][:, 3, 0, 0:1], 0.0)
-        late_flat = sig[1][:].rearrange("p t l c -> p (t l c)")
-        shared = late_flat[:, HALF : HALF + S].rearrange("p (b l c) -> p l b c", b=2, l=GAMES)
-
-        def sig_place(h, t):
-            if (h, t) == (0, PACK - 1):
-                return shared
-            return sig[h][:, t, :, :].rearrange("p l (b c) -> p l b c", b=2)
-
-        diffs = [keep.tile([P, PACK, GAMES, HALF], F32, name="diffs", tag=tag) for tag in ("diffs_early", "diffs_late")]
-
-        def sigmoids(h, t, scale=STEP, bias=0.0, pieces=(slice(0, GAMES),)):
-            diff = diffs[h][:, t, :, :]
-            for l in range(GAMES):
-                nc.vector.tensor_tensor(
-                    out=diff[:, l, :],
-                    in0=z_win[t][:].indirect(opp_t[l][:, h * HALF // GROUP : (h + 1) * HALF // GROUP]),
-                    in1=z_own[h][:, t, :],
-                    op=ALU.subtract,
-                )
-            source = diff.rearrange("p l (b c) -> p l b c", b=2)
-            for games in pieces:
-                nc.scalar.activation(
-                    out=sig_place(h, t)[:, games], in_=source[:, games], func=ACT.Sigmoid, scale=scale, bias=bias
-                )
-
-        def leave(n, scale):
-            nc.scalar.activation(out=move_t[n][:], in_=sums[n][:], func=ACT.Copy, scale=scale, bias=-STEP * GAMES)
-            return move_t[n]
-
-        def turn_back(n, turned):
-            move = psum.tile([P, len(units[n]), BLK], F32, name="move", tag="bank%d" % n)
-            for q in range(len(units[n])):
-                nc.tensor.transpose(move[:, q, :], turned[:, q, :], ident[:])
-            return move
-
+        for t in range(3):
+            window(t)
+        add_rows(0, 0, rating(0, 0), start=True)
+        for t in range(2):
+            add_rows(0, t, result(0, t, 0))
+        add_rows(0, 1, rating(1, 0))
+        for t in range(2):
+            add_rows(0, t, result(1, t, 0))
+        for t in (2, 3):
+            add_rows(1, t, result(0, t, 0), start=t == 2)
+        add_rows(1, 2, rating(2, 0))
+        for t in (2, 3):
+            add_rows(1, t, result(1, t, 0))
+        sig0 = sigmoids(0, 0, sig_tile("sig_a"))
+        window(3)
+        add_sigmoids(0, 0, sig0)
+        sig1 = sigmoids(0, 1, sig_tile("sig_b"))
+        add_sigmoids(0, 1, sig1, stop=True)
+        add_rows(1, 3, rating(3, 0))
+        sig2 = sigmoids(0, 2, sig_tile("sig_c"))
+        turned0 = leave(0)
+        add_sigmoids(1, 2, sig2)
+        back0 = turn_back(0, turned0)
+        sig3 = sigmoids(0, 3, sig_tile("sig_b"))
+        finish(0, back0)
+        add_sigmoids(1, 3, sig3, stop=True)
+        sums.append(psum.tile([P, 2, 2, P], F32, name="sums", tag="bank5"))
+        add_rows(2, 0, rating(0, 1), start=True)
+        add_rows(2, 1, rating(1, 1))
+        add_rows(2, 1, res_sum[:, 0, :])
+        turned1 = leave(1)
+        sig4 = sigmoids(1, 0, sig_tile("turned0"))
+        back1 = turn_back(1, turned1)
         for l in range(GAMES):
-            for q in (2 * l, 2 * l + 1):
-                for n in range(2):
-                    add_rating(n, q)
-            for n in range(2):
-                add_result(n, l)
-        for t in range(PACK - 1):
-            sigmoids(0, t)
-        base = keep.tile([P, REST, HALF], F32, name="base")
-        nc.scalar.activation(out=base[:], in_=res_sum[:], func=ACT.Copy, scale=STEP)
-        sigmoids(0, PACK - 1)
-        add_sigmoids(0, 0)
-        add_sigmoids(1, 0)
-        for n in range(2):
-            for q in range(1, PACK):
-                add_sigmoids(n, q)
-        move_t0 = leave(0, STEP)
-        move0 = turn_back(0, move_t0)
-        sigmoids(1, 0)
-        sums.append(psum.tile([P, len(units[2]), P], F32, name="sums", tag="bank5"))
-        for q in range(len(units[2])):
-            add_rating(2, q)
-        for l in range(GAMES):
-            add_result(2, l)
-        move1 = turn_back(1, leave(1, STEP))
-        for q in range(len(units[2])):
-            add_sigmoids(2, q)
-        sigmoids(1, 1, step_held, zero_held)
-        nc.scalar.copy(out=early[:, :, 0:BLK], in_=move0[:])
-        sigmoids(1, 2)
-        nc.scalar.copy(out=early[:, :, BLK:HALF], in_=move1[:])
-        nc.sync.dma_start(out=out_rows[:, :, 0:HALF], in_=early[:])
-        move2 = turn_back(2, leave(2, STEP))
-        sigmoids(1, 3, pieces=(slice(0, 1), slice(1, 2)))
-        nc.scalar.copy(out=late[:, 0:CUT, :].rearrange("p t c -> p (t c)"), in_=move2[:].rearrange("p q c -> p (q c)"))
+            add_rows(2, 0, result(l, 0, 1))
+        add_sigmoids(2, 0, sig4)
+        sig5 = sigmoids(1, 1, sig_tile("sig_b"))
+        finish(1, back1)
+        add_sigmoids(2, 1, sig5, stop=True)
+        sig_last = keep.tile([P, 2, GAMES, HALF], F32, name="sig_last", tag="turned1")
+        sigmoids(1, 2, sig_last[:, 0])
+        back2 = turn_back(2, leave(2))
+        sigmoids(1, 3, sig_last[:, 1], pieces=(slice(0, 1), slice(1, 2)))
         round_columns(0, BLK, nc.scalar.copy)
+        finish(2, back2)
         round_columns(BLK, HALF, nc.scalar.copy)
 
         def add_scaled(out, term, before):
             nc.vector.scalar_tensor_tensor(out=out, in0=term, scalar=STEP, in1=before, op0=ALU.mult, op1=ALU.add)
 
-        with_z = keep.tile([P, REST, HALF], F32, name="with_z", tag="z_win%d" % (PACK - 2))
-        with_one = keep.tile([P, REST, HALF], F32, name="with_one")
-        one_row, two_rows = slice(0, 1), slice(1, REST)
-        for rows in (one_row, two_rows):
-            add_scaled(with_z[:, rows, :], z_own[1][:, CUT:PACK, :][:, rows, :], base[:, rows, :])
-        pieces = ((one_row, slice(0, HALF)), (two_rows, slice(0, BLK)), (two_rows, slice(BLK, HALF)))
-        for before, after, l in ((with_z, with_one, 0), (with_one, late[:, CUT:PACK, :], 1)):
-            for rows, cols in pieces:
-                add_scaled(after[:, rows, cols], sig[1][:, CUT:PACK, l, :][:, rows, cols], before[:, rows, cols])
-        for rows in (slice(0, 2), slice(2, PACK)):
-            nc.sync.dma_start(out=out_rows[:, rows, HALF:S], in_=late[:, rows, :])
+        with_y = keep.tile([P, PACK - 1, HALF], F32, name="with_y", tag="z_win%d" % (PACK - 2))
+        with_one = keep.tile([P, PACK - 1, HALF], F32, name="with_one")
+        add_scaled(with_y[:, 0, BLK:HALF], res_sum[:, 0, BLK:HALF], y_ps[len(parts) - 3][:, HALF + BLK : S])
+        for r in range(1, PACK - 1):
+            add_scaled(with_y[:, r, :], res_sum[:, r, :], y_ps[len(parts) - 3 + r][:, HALF:S])
+        for before, after, l in ((with_y, with_one, 0), (with_one, halves[1][:, 1:PACK, :], 1)):
+            add_scaled(after[:, 0, BLK:HALF], sig5[:, l, BLK:HALF], before[:, 0, BLK:HALF])
+            for cols in (slice(0, BLK), slice(BLK, HALF)):
+                add_scaled(after[:, 1:, cols], sig_last[:, :, l, cols], before[:, 1:, cols])
+        store_rows(0, 1)
+        store_rows(2, 1)
         round_columns(HALF, HALF + BLK, nc.scalar.copy)
+        round_columns(HALF + BLK, S, nc.vector.tensor_copy)
         quantize(0, HALF)
         store_codes(0, HALF)
-        round_columns(HALF + BLK, S, nc.vector.tensor_copy)
         quantize(HALF, HALF + BLK)
         quantize(HALF + BLK, S)
         store_codes(HALF, S)

@@ -76,12 +76,18 @@ def tile_picked_elo8_none_po_kernel(
             nc.sync.dma_start(out=xs[i:P:32, :].bitcast(I32), in_=xs_picked[spread * i : P : 32, :].bitcast(I32))
         nc.sync.dma_start(out=xw_raw[1][:].bitcast(I32), in_=word_rows[1])
         res_rows = [res.rearrange("(p t) n -> p t n", t=PACK) for res in (res1, res2)]
-        res_half = [[keep.tile([P, PACK, HALF], F32, name="res%d_%d" % (l, h)) for h in range(2)] for l in range(GAMES)]
+        res_late = [keep.tile([P, 2, HALF], F32, name="res_late%d" % l) for l in range(GAMES)]
+        res_row = [[keep.tile([P, S], F32, name="res_row%d_%d" % (l, t)) for t in range(2)] for l in range(GAMES)]
+        res_mid = [keep.tile([P, 2, HALF], F32, name="res_mid%d" % l) for l in range(GAMES)]
         nc.sync.dma_start(out=opp_t[0][:], in_=opp1)
         nc.sync.dma_start(out=opp_t[1][:], in_=opp2)
-        for h, t0, t1 in ((1, 1, 2), (1, 2, PACK), (0, 0, 2), (0, 2, PACK), (1, 0, 1)):
+        for l in range(GAMES):
+            nc.sync.dma_start(out=res_late[l][:], in_=res_rows[l][:, 2:PACK, HALF:S])
+        for t in range(2):
             for l in range(GAMES):
-                nc.sync.dma_start(out=res_half[l][h][:, t0:t1, :], in_=res_rows[l][:, t0:t1, h * HALF : (h + 1) * HALF])
+                nc.sync.dma_start(out=res_row[l][t][:], in_=res_rows[l][:, t, :])
+        for l in range(GAMES):
+            nc.sync.dma_start(out=res_mid[l][:], in_=res_rows[l][:, 2:PACK, 0:HALF])
 
         w_bf = [keep.tile([P, PACK * N], BF16, name="w_bf%d" % g, align_bytes=64) for g in range(PASSES)]
         w_codes = [keep.tile([P, N], U32, name="w_codes%d" % g, align_bytes=64) for g in range(PASSES)]
@@ -97,17 +103,9 @@ def tile_picked_elo8_none_po_kernel(
 
         prepare_w(0)
 
-        pieces_x = ((0, HALF), (HALF, S))
-        parts = [(0, c0, c1) for c0, c1 in pieces_x] + [(t, 0, S) for t in range(1, PACK)]
-        part_banks = (0, 1, 2, 3, 4)
-        y_ps = {}
-
-        def product(g, i):
-            t, c0, c1 = parts[i]
-            if g == 0:
-                y_ps[i] = psum.tile([P, c1 - c0], F32, name="y_ps%d" % i, tag="bank%d" % part_banks[i])
+        def product(out, g, t, c0, c1):
             nc.tensor.matmul_mx(
-                out=y_ps[i][:],
+                out=out,
                 lhsT=w_codes[g][:, t * P : (t + 1) * P].bitcast(FP8X4),
                 lhsT_scale=w_sc[g][:, t * P : (t + 1) * P],
                 rhs=xw[g][:, c0:c1].bitcast(FP8X4),
@@ -116,120 +114,122 @@ def tile_picked_elo8_none_po_kernel(
                 stop=(g == PASSES - 1),
             )
 
+        y0 = [psum.tile([P, HALF], F32, name="y0_%d" % h, tag="bank%d" % h) for h in range(2)]
+        y1 = psum.tile([P, S], F32, name="y1", tag="bank2")
         nc.vector.tensor_copy(out=xw[0][:], in_=xw_raw[0][:].indirect(offs_t[:]))
-        for i in range(len(parts)):
-            product(0, i)
+        for h in range(2):
+            product(y0[h][:], 0, 0, h * HALF, (h + 1) * HALF)
+        y2 = psum.tile([P, S], F32, name="y2", tag="bank6")
+        y3 = psum.tile([P, S], F32, name="y3", tag="bank7")
+        for t, bank in ((1, y1), (2, y2), (3, y3)):
+            product(bank[:], 0, t, 0, S)
         prepare_w(1)
         for c0, c1 in ((0, HALF), (HALF, S)):
             nc.vector.tensor_copy(out=xw[1][:, c0:c1], in_=xw_raw[1][:].indirect(offs_t[:, c0 // GROUP : c1 // GROUP]))
 
-        res_sum = keep.tile([P, PACK - 1, HALF], F32, name="res_sum")
-        minus_games = keep.tile([P, 1], F32, name="minus_games", tag="diffs_early")
-        nc.gpsimd.memset(minus_games[:], -float(GAMES))
-        sums_of_results = (
-            (0, slice(0, BLK), 0.0),
-            (0, slice(BLK, HALF), -float(GAMES)),
-            (1, slice(0, HALF), minus_games[:]),
-            (2, slice(0, HALF), -float(GAMES)),
-        )
-        for r, cols, scalar in sums_of_results:
+        res_sum = keep.tile([P, 2, HALF], F32, name="res_sum")
+        for i, (r, cols) in enumerate(((0, slice(0, HALF)), (1, slice(0, BLK)), (1, slice(BLK, HALF)))):
+            minus_games = keep.tile([P, 1], F32, name="minus_games", tag="diffs%d" % i)
+            nc.gpsimd.memset(minus_games[:], -float(GAMES))
             nc.vector.scalar_tensor_tensor(
                 out=res_sum[:, r, cols],
-                in0=res_half[0][1][:, 1 + r, cols],
-                scalar=scalar,
-                in1=res_half[1][1][:, 1 + r, cols],
+                in0=res_late[0][:, r, cols],
+                scalar=minus_games[:],
+                in1=res_late[1][:, r, cols],
                 op0=ALU.add,
                 op1=ALU.add,
             )
 
-        z_win = [keep.tile([P, S], F32, name="z_win%d" % t, tag="z_win%d" % t) for t in range(PACK)]
-        z_own = [keep.tile([P, PACK, HALF], F32, name="z_own%d" % h) for h in range(2)]
+        slots = ((0, 0), (0, 1), (1, 0), (1, 1), (2, 0), (3, 0), (2, 1), (3, 1))
+        turned_slots = 6
+        sig = [keep.tile([P, GAMES, HALF], F32, name="sig%d" % k)[:] for k in range(turned_slots)]
+        sig_last = keep.tile([P, 2, GAMES, HALF], F32, name="sig_last")
+        sig = sig + [sig_last[:, 0], sig_last[:, 1]]
+        steps = [sig[k + 2][:, 0, 0:1] for k in range(turned_slots)]
+        for step in steps:
+            nc.gpsimd.memset(step, STEP)
 
-        def window(t):
-            for i, (row, c0, c1) in enumerate(parts):
-                if row == t:
-                    nc.scalar.activation(out=z_win[t][:, c0:c1], in_=y_ps[i][:], func=ACT.Copy, scale=1.0 / STEP)
-                    if c0 == 0:
-                        nc.scalar.activation(out=z_own[0][:, t, :], in_=y_ps[i][:, 0:HALF], func=ACT.Copy, scale=1.0 / STEP)
-            nc.sync.dma_start(out=z_own[1][:, t, :], in_=z_win[t][:, HALF:S])
+        z_win = [keep.tile([P, S], F32, name="z_win%d" % t) for t in range(PACK)]
+        z_own = [keep.tile([P, S], F32, name="z_own%d" % t) for t in range(PACK)]
 
-        for i in range(len(parts)):
-            product(1, i)
+        def to_z(out, bank):
+            nc.scalar.activation(out=out, in_=bank, func=ACT.Copy, scale=1.0 / STEP)
 
-        groups = ((0, 0), (2, 0), (0, 1))
-        sums = [psum.tile([P, 2, 2, P], F32, name="sums", tag="bank%d" % bank) for bank in (5, 6)]
+        for h in range(2):
+            product(y0[h][:], 1, 0, h * HALF, (h + 1) * HALF)
+        for t, bank in ((1, y1), (2, y2), (3, y3)):
+            product(bank[:], 1, t, 0, S)
+        for h in range(2):
+            to_z(z_win[0][:, h * HALF : (h + 1) * HALF], y0[h][:])
+            to_z(z_own[0][:, h * HALF : (h + 1) * HALF], y0[h][:])
+        to_z(z_win[1][:], y1[:])
+        nc.sync.dma_start(out=z_own[1][:, HALF:S], in_=z_win[1][:, HALF:S])
+        to_z(z_own[1][:, 0:HALF], y1[:, 0:HALF])
 
-        def blocks(n, r):
-            return range(1 if (n, r) == (2, 1) else 2)
+        sum_banks = (3, 4, 5, 0, 1, 2)
+        sums = [psum.tile([P, 2, P], F32, name="sums%d" % k, tag="bank%d" % sum_banks[k]) for k in range(turned_slots)]
 
-        def add_rows(n, t, term, start=False, stop=False):
-            for b in blocks(n, t - groups[n][0]):
+        def add_rows(k, term, start=False, stop=False):
+            for b in range(2):
                 nc.tensor.matmul(
-                    out=sums[n][:, t - groups[n][0], b, :],
+                    out=sums[k][:, b, :],
                     lhsT=term[:, b * BLK : (b + 1) * BLK],
                     rhs=ident[:],
                     start=start and b == 0,
-                    stop=stop and b == blocks(n, t - groups[n][0])[-1],
+                    stop=stop and b == 1,
                     is_transpose=True,
                 )
 
-        def rating(t, h):
-            return z_win[t][:, h * HALF : (h + 1) * HALF]
-
         def result(l, t, h):
-            return res_half[l][h][:, t, :]
+            return res_row[l][t][:, h * HALF : (h + 1) * HALF] if t < 2 else res_mid[l][:, t - 2, :]
 
-        diffs = [keep.tile([P, PACK, GAMES, HALF], F32, name="diffs", tag=tag) for tag in ("diffs_early", "diffs_late")]
+        def add_rating(k, start=False):
+            t, h = slots[k]
+            add_rows(k, z_win[t][:, h * HALF : (h + 1) * HALF], start=start)
 
-        def differences(h, t):
+        def add_results(k, start=False):
+            t, h = slots[k]
+            for l in range(GAMES):
+                add_rows(k, result(l, t, h), start=start and l == 0)
+
+        def sigmoids(k, pieces=(slice(0, GAMES),)):
+            t, h = slots[k]
+            diffs = keep.tile([P, GAMES, HALF], F32, name="diffs", tag="diffs%d" % (0, 1, 2, 0, 1, 2, 1, 2)[k])
             for l in range(GAMES):
                 nc.vector.tensor_tensor(
-                    out=diffs[h][:, t, l, :],
+                    out=diffs[:, l, :],
                     in0=z_win[t][:].indirect(opp_t[l][:, h * HALF // GROUP : (h + 1) * HALF // GROUP]),
-                    in1=z_own[h][:, t, :],
+                    in1=z_own[t][:, h * HALF : (h + 1) * HALF],
                     op=ALU.subtract,
                 )
-
-        def sigmoids(h, t, out, pieces=(slice(0, GAMES),)):
-            differences(h, t)
             for games in pieces:
-                nc.scalar.activation(out=out[:, games, :], in_=diffs[h][:, t, games, :], func=ACT.Sigmoid, scale=STEP)
-            return out
+                nc.scalar.activation(out=sig[k][:, games, :], in_=diffs[:, games, :], func=ACT.Sigmoid, scale=STEP)
+            return diffs
 
-        def sig_tile(tag):
-            return keep.tile([P, GAMES, HALF], F32, name="sig", tag=tag)[:]
-
-        def add_sigmoids(n, t, sig, stop=False):
+        def add_sigmoids(k):
             for l in range(GAMES):
-                add_rows(n, t, sig[:, l, :], stop=stop and l == GAMES - 1)
+                add_rows(k, sig[k][:, l, :], stop=l == GAMES - 1)
 
-        def used(n, tile):
-            return tile[:].rearrange("p r b c -> p (r b c)")[:, 0 : (3 if n == 2 else 4) * BLK]
+        turned = [keep.tile([P, 2, P], F32, name="turned%d" % k) for k in range(turned_slots)]
+        backs = {}
 
-        def leave(n):
-            turned = keep.tile([P, 2, 2, P], F32, name="turned", tag="turned%d" % n)
-            nc.scalar.activation(out=used(n, turned), in_=used(n, sums[n]), func=ACT.Copy, scale=STEP, bias=-STEP * GAMES)
-            return turned
+        def leave(k):
+            nc.scalar.activation(out=turned[k][:], in_=sums[k][:], func=ACT.Copy, scale=steps[k], bias=-STEP * GAMES)
 
-        def turn_back(n, turned):
-            back = psum.tile([P, 2, 2, BLK], F32, name="back", tag="bank%d" % (0, 1, 7)[n])
-            for r in range(2):
-                for b in blocks(n, r):
-                    nc.tensor.transpose(back[:, r, b, :], turned[:, r, b, :], ident[:])
-            return back
+        def turn_back(k):
+            backs[k] = psum.tile([P, 2, BLK], F32, name="back%d" % k, tag="bank%d" % sum_banks[k])
+            for b in range(2):
+                nc.tensor.transpose(backs[k][:, b, :], turned[k][:, b, :], ident[:])
 
-        halves = [keep.tile([P, PACK, HALF], F32, name="half%d" % h) for h in range(2)]
+        rows = keep.tile([P, PACK, S], F32, name="rows")
         out_rows = out_0.rearrange("(p t) n -> p t n", t=PACK)
 
-        def store_rows(t0, h):
-            nc.sync.dma_start(out=out_rows[:, t0 : t0 + 2, h * HALF : (h + 1) * HALF], in_=halves[h][:, t0 : t0 + 2, :])
+        def finish(k):
+            t, h = slots[k]
+            nc.scalar.copy(out=rows[:, t, h * HALF : (h + 1) * HALF], in_=backs[k][:].rearrange("p b c -> p (b c)"))
 
-        def finish(n, back):
-            t0, h = groups[n]
-            place = halves[h][:, t0 : t0 + 2, :].rearrange("p r c -> p (r c)")
-            nc.scalar.copy(out=place[:, 0 : (3 if n == 2 else 4) * BLK], in_=used(n, back))
-            if n < 2:
-                store_rows(t0, h)
+        def store_rows(t0, t1, c0, c1):
+            nc.sync.dma_start(out=out_rows[:, t0:t1, c0:c1], in_=rows[:, t0:t1, c0:c1])
 
         o_codes = keep.tile([P, S], U32, name="o_codes", align_bytes=64)
         o_sc = keep.tile([P, S], U8, name="o_sc", align_bytes=64)
@@ -239,7 +239,7 @@ def tile_picked_elo8_none_po_kernel(
         def round_columns(c0, c1, copy):
             copy(
                 out=rounded[:, c0 * PACK : c1 * PACK].rearrange("p (c i t) -> p c t i", i=4, t=PACK),
-                in_=halves[c0 // HALF][:, :, c0 % HALF : (c1 - 1) % HALF + 1].rearrange("p t (c i) -> p c t i", i=4),
+                in_=rows[:, :, c0:c1].rearrange("p t (c i) -> p c t i", i=4),
             )
 
         def quantize(c0, c1):
@@ -250,73 +250,63 @@ def tile_picked_elo8_none_po_kernel(
         def store_codes(c0, c1):
             nc.sync.dma_start(out=out_words[:, c0:c1], in_=o_codes[:, c0:c1].bitcast(I32))
 
-        for t in range(3):
-            window(t)
-        add_rows(0, 0, rating(0, 0), start=True)
-        for t in range(2):
-            add_rows(0, t, result(0, t, 0))
-        add_rows(0, 1, rating(1, 0))
-        for t in range(2):
-            add_rows(0, t, result(1, t, 0))
-        for t in (2, 3):
-            add_rows(1, t, result(0, t, 0), start=t == 2)
-        add_rows(1, 2, rating(2, 0))
-        for t in (2, 3):
-            add_rows(1, t, result(1, t, 0))
-        sig0 = sigmoids(0, 0, sig_tile("sig_a"))
-        window(3)
-        add_sigmoids(0, 0, sig0)
-        sig1 = sigmoids(0, 1, sig_tile("sig_b"))
-        add_sigmoids(0, 1, sig1, stop=True)
-        add_rows(1, 3, rating(3, 0))
-        sig2 = sigmoids(0, 2, sig_tile("sig_c"))
-        turned0 = leave(0)
-        add_sigmoids(1, 2, sig2)
-        back0 = turn_back(0, turned0)
-        sig3 = sigmoids(0, 3, sig_tile("sig_b"))
-        finish(0, back0)
-        add_sigmoids(1, 3, sig3, stop=True)
-        sums.append(psum.tile([P, 2, 2, P], F32, name="sums", tag="bank5"))
-        add_rows(2, 0, rating(0, 1), start=True)
-        add_rows(2, 1, rating(1, 1))
-        add_rows(2, 1, res_sum[:, 0, :])
-        turned1 = leave(1)
-        sig4 = sigmoids(1, 0, sig_tile("turned0"))
-        back1 = turn_back(1, turned1)
-        for l in range(GAMES):
-            add_rows(2, 0, result(l, 0, 1))
-        add_sigmoids(2, 0, sig4)
-        sig5 = sigmoids(1, 1, sig_tile("sig_b"))
-        finish(1, back1)
-        add_sigmoids(2, 1, sig5, stop=True)
-        sig_last = keep.tile([P, 2, GAMES, HALF], F32, name="sig_last", tag="turned1")
-        sigmoids(1, 2, sig_last[:, 0])
-        back2 = turn_back(2, leave(2))
-        sigmoids(1, 3, sig_last[:, 1], pieces=(slice(0, 1), slice(1, 2)))
+        add_rating(0, start=True)
+        add_results(0)
+        add_rating(1, start=True)
+        add_results(1)
+        to_z(z_win[2][:], y2[:])
+        nc.sync.dma_start(out=z_own[2][:], in_=z_win[2][:])
+        add_rating(2, start=True)
+        add_results(2)
+        d0 = sigmoids(0)
+        to_z(z_win[3][:], y3[:])
+        nc.sync.dma_start(out=z_own[3][:], in_=z_win[3][:])
+        add_sigmoids(0)
+        add_rating(3, start=True)
+        add_results(3)
+        sigmoids(1)
+        add_sigmoids(1)
+        leave(0)
+        turn_back(0)
+        add_rating(4, start=True)
+        add_results(4)
+        sigmoids(2)
+        add_sigmoids(2)
+        leave(1)
+        finish(0)
+        turn_back(1)
+        add_rating(5, start=True)
+        add_results(5)
+        for k in range(3, 8):
+            sigmoids(k, pieces=(slice(0, 1), slice(1, 2)) if k == 7 else (slice(0, GAMES),))
+            if k < turned_slots:
+                add_sigmoids(k)
+            if k - 1 < turned_slots:
+                leave(k - 1)
+                turn_back(k - 1)
+            finish(k - 2)
+            if k - 2 in (1, 3):
+                store_rows((k - 2) // 2, (k - 2) // 2 + 1, 0, S)
+        store_rows(2, PACK, 0, HALF)
         round_columns(0, BLK, nc.scalar.copy)
-        finish(2, back2)
         round_columns(BLK, HALF, nc.scalar.copy)
 
         def add_scaled(out, term, before):
             nc.vector.scalar_tensor_tensor(out=out, in0=term, scalar=STEP, in1=before, op0=ALU.mult, op1=ALU.add)
 
-        with_y = keep.tile([P, PACK - 1, HALF], F32, name="with_y", tag="z_win%d" % (PACK - 2))
-        with_one = keep.tile([P, PACK - 1, HALF], F32, name="with_one")
-        add_scaled(with_y[:, 0, BLK:HALF], res_sum[:, 0, BLK:HALF], y_ps[len(parts) - 3][:, HALF + BLK : S])
-        for r in range(1, PACK - 1):
-            add_scaled(with_y[:, r, :], res_sum[:, r, :], y_ps[len(parts) - 3 + r][:, HALF:S])
-        for before, after, l in ((with_y, with_one, 0), (with_one, halves[1][:, 1:PACK, :], 1)):
-            add_scaled(after[:, 0, BLK:HALF], sig5[:, l, BLK:HALF], before[:, 0, BLK:HALF])
+        with_y = keep.tile([P, 2, HALF], F32, name="with_y", tag="diffs1")
+        with_one = keep.tile([P, 2, HALF], F32, name="with_one")
+        for r, bank in ((0, y2), (1, y3)):
+            add_scaled(with_y[:, r, :], res_sum[:, r, :], bank[:, HALF:S])
+        for before, after, l in ((with_y[:], with_one[:], 0), (with_one[:], rows[:, 2:PACK, HALF:S], 1)):
             for cols in (slice(0, BLK), slice(BLK, HALF)):
-                add_scaled(after[:, 1:, cols], sig_last[:, :, l, cols], before[:, 1:, cols])
-        store_rows(0, 1)
-        store_rows(2, 1)
-        round_columns(HALF, HALF + BLK, nc.scalar.copy)
+                add_scaled(after[:, :, cols], sig_last[:, :, l, cols], before[:, :, cols])
+        store_rows(2, PACK, HALF, S)
+        round_columns(HALF, HALF + BLK, nc.vector.tensor_copy)
         round_columns(HALF + BLK, S, nc.vector.tensor_copy)
         quantize(0, HALF)
         store_codes(0, HALF)
-        quantize(HALF, HALF + BLK)
-        quantize(HALF + BLK, S)
+        quantize(HALF, S)
         store_codes(HALF, S)
         for q in range(QUADS):
             queue = nc.scalar if q % 2 else nc.sync

@@ -77,17 +77,17 @@ def tile_picked_elo8_none_po_kernel(
         nc.sync.dma_start(out=xw_raw[1][:].bitcast(I32), in_=word_rows[1])
         res_rows = [res.rearrange("(p t) n -> p t n", t=PACK) for res in (res1, res2)]
         res_late = [keep.tile([P, 2, HALF], F32, name="res_late%d" % l) for l in range(GAMES)]
-        res_row = [[keep.tile([P, S], F32, name="res_row%d_%d" % (l, t)) for t in range(2)] for l in range(GAMES)]
-        res_mid = [keep.tile([P, 2, HALF], F32, name="res_mid%d" % l) for l in range(GAMES)]
+        res_row = [[keep.tile([P, S], F32, name="res_row%d_%d" % (l, t), tag="res_row%d_%d" % (l, t)) for t in range(2)] for l in range(GAMES)]
+        res_mid = [keep.tile([P, 2, HALF], F32, name="res_mid%d" % l, tag="res_mid%d" % l) for l in range(GAMES)]
         nc.sync.dma_start(out=opp_t[0][:], in_=opp1)
         nc.sync.dma_start(out=opp_t[1][:], in_=opp2)
         for l in range(GAMES):
-            nc.sync.dma_start(out=res_late[l][:], in_=res_rows[l][:, 2:PACK, HALF:S])
+            nc.sync.dma_start(out=res_late[l][:], in_=res_rows[l][:, 2:PACK, 0:HALF])
         for t in range(2):
             for l in range(GAMES):
                 nc.sync.dma_start(out=res_row[l][t][:], in_=res_rows[l][:, t, :])
         for l in range(GAMES):
-            nc.sync.dma_start(out=res_mid[l][:], in_=res_rows[l][:, 2:PACK, 0:HALF])
+            nc.sync.dma_start(out=res_mid[l][:], in_=res_rows[l][:, 2:PACK, HALF:S])
 
         w_bf = [keep.tile([P, PACK * N], BF16, name="w_bf%d" % g, align_bytes=64) for g in range(PASSES)]
         w_codes = [keep.tile([P, N], U32, name="w_codes%d" % g, align_bytes=64) for g in range(PASSES)]
@@ -103,15 +103,15 @@ def tile_picked_elo8_none_po_kernel(
 
         prepare_w(0)
 
-        def product(out, g, t, c0, c1):
+        def product(out, g, t, c0, c1, start=True, stop=True):
             nc.tensor.matmul_mx(
                 out=out,
                 lhsT=w_codes[g][:, t * P : (t + 1) * P].bitcast(FP8X4),
                 lhsT_scale=w_sc[g][:, t * P : (t + 1) * P],
                 rhs=xw[g][:, c0:c1].bitcast(FP8X4),
                 rhs_scale=xs[:, g * S + c0 : g * S + c1],
-                start=(g == 0),
-                stop=(g == PASSES - 1),
+                start=start and g == 0,
+                stop=stop and g == PASSES - 1,
             )
 
         y0 = [psum.tile([P, HALF], F32, name="y0_%d" % h, tag="bank%d" % h) for h in range(2)]
@@ -119,46 +119,59 @@ def tile_picked_elo8_none_po_kernel(
         nc.vector.tensor_copy(out=xw[0][:], in_=xw_raw[0][:].indirect(offs_t[:]))
         for h in range(2):
             product(y0[h][:], 0, 0, h * HALF, (h + 1) * HALF)
-        y2 = psum.tile([P, S], F32, name="y2", tag="bank6")
-        y3 = psum.tile([P, S], F32, name="y3", tag="bank7")
-        for t, bank in ((1, y1), (2, y2), (3, y3)):
-            product(bank[:], 0, t, 0, S)
+        y23 = [psum.tile([P, 2, HALF], F32, name="y23_%d" % h, tag="bank%d" % (6 + h)) for h in range(2)]
+        product(y1[:], 0, 1, 0, S)
+        for h in range(2):
+            for r in range(2):
+                product(y23[h][:, r, :], 0, 2 + r, h * HALF, (h + 1) * HALF, start=r == 0)
         prepare_w(1)
         for c0, c1 in ((0, HALF), (HALF, S)):
             nc.vector.tensor_copy(out=xw[1][:, c0:c1], in_=xw_raw[1][:].indirect(offs_t[:, c0 // GROUP : c1 // GROUP]))
 
-        res_sum = keep.tile([P, 2, HALF], F32, name="res_sum")
-        for i, (r, cols) in enumerate(((0, slice(0, HALF)), (1, slice(0, BLK)), (1, slice(BLK, HALF)))):
-            minus_games = keep.tile([P, 1], F32, name="minus_games", tag="diffs%d" % i)
-            nc.gpsimd.memset(minus_games[:], -float(GAMES))
+        product(y0[0][:], 1, 0, 0, HALF)
+        product(y23[0][:, 0, :], 1, 2, 0, HALF, stop=False)
+        product(y23[0][:, 1, :], 1, 3, 0, HALF)
+        product(y0[1][:], 1, 0, HALF, S)
+        product(y1[:], 1, 1, 0, S)
+        for r in range(2):
+            product(y23[1][:, r, :], 1, 2 + r, HALF, S, stop=r == 1)
+
+        def add_scaled(out, term, before, step=STEP):
+            nc.vector.scalar_tensor_tensor(out=out, in0=term, scalar=step, in1=before, op0=ALU.mult, op1=ALU.add)
+
+        res_sum = [keep.tile([P, HALF], F32, name="res_sum%d" % r, tag="z_win%d" % (2 + r)) for r in range(2)]
+        for r in range(2):
             nc.vector.scalar_tensor_tensor(
-                out=res_sum[:, r, cols],
-                in0=res_late[0][:, r, cols],
-                scalar=minus_games[:],
-                in1=res_late[1][:, r, cols],
+                out=res_sum[r][:],
+                in0=res_late[0][:, r, :],
+                scalar=-float(GAMES),
+                in1=res_late[1][:, r, :],
                 op0=ALU.add,
                 op1=ALU.add,
             )
+        with_y = keep.tile([P, 2, HALF], F32, name="with_y")
+        first_step = keep.tile([P, 1], F32, name="first_step", tag="diffs")
+        nc.gpsimd.memset(first_step[:], STEP)
+        add_scaled(with_y[:, 0, :], res_sum[0][:], y23[0][:, 0, :], step=first_step[:])
+        add_scaled(with_y[:, 1, :], res_sum[1][:], y23[0][:, 1, :])
 
-        slots = ((0, 0), (0, 1), (1, 0), (1, 1), (2, 0), (3, 0), (2, 1), (3, 1))
+        all_diffs = keep.tile([P, 3, GAMES, HALF], F32, name="diffs", tag="diffs")
+        slots = ((0, 0), (0, 1), (1, 0), (1, 1), (2, 1), (3, 1), (2, 0), (3, 0))
         turned_slots = 6
-        sig = [keep.tile([P, GAMES, HALF], F32, name="sig%d" % k)[:] for k in range(turned_slots)]
+        sig = [None, None] + [keep.tile([P, GAMES, HALF], F32, name="sig%d" % k)[:] for k in range(2, turned_slots)]
         sig_last = keep.tile([P, 2, GAMES, HALF], F32, name="sig_last")
         sig = sig + [sig_last[:, 0], sig_last[:, 1]]
-        steps = [sig[k + 2][:, 0, 0:1] for k in range(turned_slots)]
+        steps = [sig[k + 2][:, 0, 0:1] for k in range(turned_slots - 1)]
         for step in steps:
             nc.gpsimd.memset(step, STEP)
+        steps.append(STEP)
 
-        z_win = [keep.tile([P, S], F32, name="z_win%d" % t) for t in range(PACK)]
+        z_win = [keep.tile([P, S], F32, name="z_win%d" % t, tag="z_win%d" % t) for t in range(PACK)]
         z_own = [keep.tile([P, S], F32, name="z_own%d" % t) for t in range(PACK)]
 
         def to_z(out, bank):
             nc.scalar.activation(out=out, in_=bank, func=ACT.Copy, scale=1.0 / STEP)
 
-        for h in range(2):
-            product(y0[h][:], 1, 0, h * HALF, (h + 1) * HALF)
-        for t, bank in ((1, y1), (2, y2), (3, y3)):
-            product(bank[:], 1, t, 0, S)
         for h in range(2):
             to_z(z_win[0][:, h * HALF : (h + 1) * HALF], y0[h][:])
             to_z(z_own[0][:, h * HALF : (h + 1) * HALF], y0[h][:])
@@ -187,14 +200,14 @@ def tile_picked_elo8_none_po_kernel(
             t, h = slots[k]
             add_rows(k, z_win[t][:, h * HALF : (h + 1) * HALF], start=start)
 
-        def add_results(k, start=False):
-            t, h = slots[k]
-            for l in range(GAMES):
-                add_rows(k, result(l, t, h), start=start and l == 0)
+        def add_results(l, ks, start=False):
+            for k in ks:
+                t, h = slots[k]
+                add_rows(k, result(l, t, h), start=start)
 
-        def sigmoids(k, pieces=(slice(0, GAMES),)):
+        def sigmoids(k, pieces=((slice(0, GAMES), STEP),)):
             t, h = slots[k]
-            diffs = keep.tile([P, GAMES, HALF], F32, name="diffs", tag="diffs%d" % (0, 1, 2, 0, 1, 2, 1, 2)[k])
+            diffs = all_diffs[:, (0, 1, 2, 0, 1, 2, 1, 2)[k]]
             for l in range(GAMES):
                 nc.vector.tensor_tensor(
                     out=diffs[:, l, :],
@@ -202,8 +215,8 @@ def tile_picked_elo8_none_po_kernel(
                     in1=z_own[t][:, h * HALF : (h + 1) * HALF],
                     op=ALU.subtract,
                 )
-            for games in pieces:
-                nc.scalar.activation(out=sig[k][:, games, :], in_=diffs[:, games, :], func=ACT.Sigmoid, scale=STEP)
+            for games, scale in pieces:
+                nc.scalar.activation(out=sig[k][:, games, :], in_=diffs[:, games, :], func=ACT.Sigmoid, scale=scale)
             return diffs
 
         def add_sigmoids(k):
@@ -222,6 +235,8 @@ def tile_picked_elo8_none_po_kernel(
                 nc.tensor.transpose(backs[k][:, b, :], turned[k][:, b, :], ident[:])
 
         rows = keep.tile([P, PACK, S], F32, name="rows")
+        last_step = rows[:, 2, 0:1]
+        nc.gpsimd.memset(last_step, STEP)
         out_rows = out_0.rearrange("(p t) n -> p t n", t=PACK)
 
         def finish(k):
@@ -251,62 +266,66 @@ def tile_picked_elo8_none_po_kernel(
             nc.sync.dma_start(out=out_words[:, c0:c1], in_=o_codes[:, c0:c1].bitcast(I32))
 
         add_rating(0, start=True)
-        add_results(0)
         add_rating(1, start=True)
-        add_results(1)
-        to_z(z_win[2][:], y2[:])
+        for l in range(GAMES):
+            add_results(l, (0, 1))
+        for l in range(GAMES):
+            add_results(l, (2, 3), start=l == 0)
+        add_rating(2)
+        add_rating(3)
+        for h in range(2):
+            to_z(z_win[2][:, h * HALF : (h + 1) * HALF], y23[h][:, 0, :])
         nc.sync.dma_start(out=z_own[2][:], in_=z_win[2][:])
-        add_rating(2, start=True)
-        add_results(2)
-        d0 = sigmoids(0)
-        to_z(z_win[3][:], y3[:])
+        for h in range(2):
+            to_z(z_win[3][:, h * HALF : (h + 1) * HALF], y23[h][:, 1, :])
         nc.sync.dma_start(out=z_own[3][:], in_=z_win[3][:])
+        add_results(0, (4, 5), start=True)
+        sig[0] = keep.tile([P, GAMES, HALF], F32, name="sig0", tag="res_row0_1")[:]
+        d0 = sigmoids(0)
+        add_results(1, (4, 5))
         add_sigmoids(0)
-        add_rating(3, start=True)
-        add_results(3)
+        add_rating(4)
+        add_rating(5)
+        sig[1] = keep.tile([P, GAMES, HALF], F32, name="sig1", tag="res_row1_1")[:]
         sigmoids(1)
         add_sigmoids(1)
         leave(0)
         turn_back(0)
-        add_rating(4, start=True)
-        add_results(4)
         sigmoids(2)
         add_sigmoids(2)
         leave(1)
         finish(0)
         turn_back(1)
-        add_rating(5, start=True)
-        add_results(5)
-        for k in range(3, 8):
-            sigmoids(k, pieces=(slice(0, 1), slice(1, 2)) if k == 7 else (slice(0, GAMES),))
+        for k in range(3, 7):
+            sigmoids(k)
             if k < turned_slots:
                 add_sigmoids(k)
-            if k - 1 < turned_slots:
-                leave(k - 1)
-                turn_back(k - 1)
-            finish(k - 2)
+            leave(k - 1)
+            turn_back(k - 1)
+            if k < turned_slots:
+                finish(k - 2)
             if k - 2 in (1, 3):
                 store_rows((k - 2) // 2, (k - 2) // 2 + 1, 0, S)
-        store_rows(2, PACK, 0, HALF)
-        round_columns(0, BLK, nc.scalar.copy)
-        round_columns(BLK, HALF, nc.scalar.copy)
-
-        def add_scaled(out, term, before):
-            nc.vector.scalar_tensor_tensor(out=out, in0=term, scalar=STEP, in1=before, op0=ALU.mult, op1=ALU.add)
-
-        with_y = keep.tile([P, 2, HALF], F32, name="with_y", tag="diffs1")
-        with_one = keep.tile([P, 2, HALF], F32, name="with_one")
-        for r, bank in ((0, y2), (1, y3)):
-            add_scaled(with_y[:, r, :], res_sum[:, r, :], bank[:, HALF:S])
-        for before, after, l in ((with_y[:], with_one[:], 0), (with_one[:], rows[:, 2:PACK, HALF:S], 1)):
-            for cols in (slice(0, BLK), slice(BLK, HALF)):
-                add_scaled(after[:, :, cols], sig_last[:, :, l, cols], before[:, :, cols])
+        sigmoids(7, pieces=((slice(0, 1), last_step), (slice(1, 2), STEP)))
+        finish(4)
+        finish(5)
         store_rows(2, PACK, HALF, S)
-        round_columns(HALF, HALF + BLK, nc.vector.tensor_copy)
-        round_columns(HALF + BLK, S, nc.vector.tensor_copy)
+        round_columns(HALF, HALF + BLK, nc.scalar.copy)
+        round_columns(HALF + BLK, S, nc.scalar.copy)
+
+        with_one = keep.tile([P, 2, HALF], F32, name="with_one")
+        for r in range(2):
+            add_scaled(with_one[:, r, :], sig_last[:, r, 0, :], with_y[:, r, :])
+        add_scaled(rows[:, 2, 0:HALF], sig_last[:, 0, 1, :], with_one[:, 0, :])
+        for cols in (slice(0, BLK), slice(BLK, HALF)):
+            add_scaled(rows[:, 3, cols], sig_last[:, 1, 1, cols], with_one[:, 1, cols])
+        store_rows(2, PACK, 0, HALF)
+        round_columns(0, BLK, nc.vector.tensor_copy)
+        round_columns(BLK, HALF, nc.vector.tensor_copy)
+        quantize(HALF, HALF + BLK)
         quantize(0, HALF)
         store_codes(0, HALF)
-        quantize(HALF, S)
+        quantize(HALF + BLK, S)
         store_codes(HALF, S)
         for q in range(QUADS):
             queue = nc.scalar if q % 2 else nc.sync

@@ -76,18 +76,12 @@ def tile_picked_elo8_none_po_kernel(
             nc.sync.dma_start(out=xs[i:P:32, :].bitcast(I32), in_=xs_picked[spread * i : P : 32, :].bitcast(I32))
         nc.sync.dma_start(out=xw_raw[1][:].bitcast(I32), in_=word_rows[1])
         res_rows = [res.rearrange("(p t) n -> p t n", t=PACK) for res in (res1, res2)]
-        res_late = [keep.tile([P, 2, HALF], F32, name="res_late%d" % l) for l in range(GAMES)]
-        res_row = [[keep.tile([P, S], F32, name="res_row%d_%d" % (l, t), tag="res_row%d_%d" % (l, t)) for t in range(2)] for l in range(GAMES)]
-        res_mid = [keep.tile([P, 2, HALF], F32, name="res_mid%d" % l, tag="res_mid%d" % l) for l in range(GAMES)]
+        res_row = [[keep.tile([P, S], F32, name="res_row%d_%d" % (l, t), tag="res_row%d_%d" % (l, t)) for t in range(PACK)] for l in range(GAMES)]
         nc.sync.dma_start(out=opp_t[0][:], in_=opp1)
         nc.sync.dma_start(out=opp_t[1][:], in_=opp2)
-        for l in range(GAMES):
-            nc.sync.dma_start(out=res_late[l][:], in_=res_rows[l][:, 2:PACK, 0:HALF])
-        for t in range(2):
+        for t in (3, 0, 1, 2):
             for l in range(GAMES):
                 nc.sync.dma_start(out=res_row[l][t][:], in_=res_rows[l][:, t, :])
-        for l in range(GAMES):
-            nc.sync.dma_start(out=res_mid[l][:], in_=res_rows[l][:, 2:PACK, HALF:S])
 
         w_bf = [keep.tile([P, PACK * N], BF16, name="w_bf%d" % g, align_bytes=64) for g in range(PASSES)]
         w_codes = [keep.tile([P, N], U32, name="w_codes%d" % g, align_bytes=64) for g in range(PASSES)]
@@ -103,15 +97,15 @@ def tile_picked_elo8_none_po_kernel(
 
         prepare_w(0)
 
-        def product(out, g, t, c0, c1, start=True, stop=True):
+        def product(out, g, t, c0, c1):
             nc.tensor.matmul_mx(
                 out=out,
                 lhsT=w_codes[g][:, t * P : (t + 1) * P].bitcast(FP8X4),
                 lhsT_scale=w_sc[g][:, t * P : (t + 1) * P],
                 rhs=xw[g][:, c0:c1].bitcast(FP8X4),
                 rhs_scale=xs[:, g * S + c0 : g * S + c1],
-                start=start and g == 0,
-                stop=stop and g == PASSES - 1,
+                start=(g == 0),
+                stop=(g == PASSES - 1),
             )
 
         y0 = [psum.tile([P, HALF], F32, name="y0_%d" % h, tag="bank%d" % h) for h in range(2)]
@@ -119,44 +113,43 @@ def tile_picked_elo8_none_po_kernel(
         nc.vector.tensor_copy(out=xw[0][:], in_=xw_raw[0][:].indirect(offs_t[:]))
         for h in range(2):
             product(y0[h][:], 0, 0, h * HALF, (h + 1) * HALF)
-        y23 = [psum.tile([P, 2, HALF], F32, name="y23_%d" % h, tag="bank%d" % (6 + h)) for h in range(2)]
-        product(y1[:], 0, 1, 0, S)
+        y2 = psum.tile([P, S], F32, name="y2", tag="bank5")
+        y3 = [psum.tile([P, HALF], F32, name="y3_%d" % h, tag="bank%d" % (6 + h)) for h in range(2)]
         for h in range(2):
-            for r in range(2):
-                product(y23[h][:, r, :], 0, 2 + r, h * HALF, (h + 1) * HALF, start=r == 0)
+            product(y3[h][:], 0, 3, h * HALF, (h + 1) * HALF)
+        product(y1[:], 0, 1, 0, S)
+        product(y2[:], 0, 2, 0, S)
         prepare_w(1)
         for c0, c1 in ((0, HALF), (HALF, S)):
             nc.vector.tensor_copy(out=xw[1][:, c0:c1], in_=xw_raw[1][:].indirect(offs_t[:, c0 // GROUP : c1 // GROUP]))
 
-        product(y0[0][:], 1, 0, 0, HALF)
-        product(y23[0][:, 0, :], 1, 2, 0, HALF, stop=False)
-        product(y23[0][:, 1, :], 1, 3, 0, HALF)
-        product(y0[1][:], 1, 0, HALF, S)
+        for h in range(2):
+            product(y0[h][:], 1, 0, h * HALF, (h + 1) * HALF)
+            product(y3[h][:], 1, 3, h * HALF, (h + 1) * HALF)
         product(y1[:], 1, 1, 0, S)
-        for r in range(2):
-            product(y23[1][:, r, :], 1, 2 + r, HALF, S, stop=r == 1)
+        product(y2[:], 1, 2, 0, S)
 
         def add_scaled(out, term, before, step=STEP):
             nc.vector.scalar_tensor_tensor(out=out, in0=term, scalar=step, in1=before, op0=ALU.mult, op1=ALU.add)
 
-        res_sum = [keep.tile([P, HALF], F32, name="res_sum%d" % r, tag="z_win%d" % (2 + r)) for r in range(2)]
-        for r in range(2):
+        res_sum = keep.tile([P, S], F32, name="res_sum", tag="z_win3")
+        for h in range(2):
             nc.vector.scalar_tensor_tensor(
-                out=res_sum[r][:],
-                in0=res_late[0][:, r, :],
+                out=res_sum[:, h * HALF : (h + 1) * HALF],
+                in0=res_row[0][3][:, h * HALF : (h + 1) * HALF],
                 scalar=-float(GAMES),
-                in1=res_late[1][:, r, :],
+                in1=res_row[1][3][:, h * HALF : (h + 1) * HALF],
                 op0=ALU.add,
                 op1=ALU.add,
             )
         with_y = keep.tile([P, 2, HALF], F32, name="with_y")
         first_step = keep.tile([P, 1], F32, name="first_step", tag="diffs")
         nc.gpsimd.memset(first_step[:], STEP)
-        add_scaled(with_y[:, 0, :], res_sum[0][:], y23[0][:, 0, :], step=first_step[:])
-        add_scaled(with_y[:, 1, :], res_sum[1][:], y23[0][:, 1, :])
+        add_scaled(with_y[:, 0, :], res_sum[:, 0:HALF], y3[0][:], step=first_step[:])
+        add_scaled(with_y[:, 1, :], res_sum[:, HALF:S], y3[1][:])
 
         all_diffs = keep.tile([P, 3, GAMES, HALF], F32, name="diffs", tag="diffs")
-        slots = ((0, 0), (0, 1), (1, 0), (1, 1), (2, 1), (3, 1), (2, 0), (3, 0))
+        slots = ((0, 0), (0, 1), (1, 0), (1, 1), (2, 0), (2, 1), (3, 0), (3, 1))
         turned_slots = 6
         sig = [None, None] + [keep.tile([P, GAMES, HALF], F32, name="sig%d" % k)[:] for k in range(2, turned_slots)]
         sig_last = keep.tile([P, 2, GAMES, HALF], F32, name="sig_last")
@@ -179,7 +172,9 @@ def tile_picked_elo8_none_po_kernel(
         nc.sync.dma_start(out=z_own[1][:, HALF:S], in_=z_win[1][:, HALF:S])
         to_z(z_own[1][:, 0:HALF], y1[:, 0:HALF])
 
-        sum_banks = (3, 4, 5, 0, 1, 2)
+        to_z(z_win[2][:], y2[:])
+        nc.sync.dma_start(out=z_own[2][:], in_=z_win[2][:])
+        sum_banks = (3, 4, 0, 1, 2, 5)
         sums = [psum.tile([P, 2, P], F32, name="sums%d" % k, tag="bank%d" % sum_banks[k]) for k in range(turned_slots)]
 
         def add_rows(k, term, start=False, stop=False):
@@ -194,7 +189,7 @@ def tile_picked_elo8_none_po_kernel(
                 )
 
         def result(l, t, h):
-            return res_row[l][t][:, h * HALF : (h + 1) * HALF] if t < 2 else res_mid[l][:, t - 2, :]
+            return res_row[l][t][:, h * HALF : (h + 1) * HALF]
 
         def add_rating(k, start=False):
             t, h = slots[k]
@@ -235,7 +230,7 @@ def tile_picked_elo8_none_po_kernel(
                 nc.tensor.transpose(backs[k][:, b, :], turned[k][:, b, :], ident[:])
 
         rows = keep.tile([P, PACK, S], F32, name="rows")
-        last_step = rows[:, 2, 0:1]
+        last_step = rows[:, 3, 0:1]
         nc.gpsimd.memset(last_step, STEP)
         out_rows = out_0.rearrange("(p t) n -> p t n", t=PACK)
 
@@ -274,10 +269,7 @@ def tile_picked_elo8_none_po_kernel(
         add_rating(2)
         add_rating(3)
         for h in range(2):
-            to_z(z_win[2][:, h * HALF : (h + 1) * HALF], y23[h][:, 0, :])
-        nc.sync.dma_start(out=z_own[2][:], in_=z_win[2][:])
-        for h in range(2):
-            to_z(z_win[3][:, h * HALF : (h + 1) * HALF], y23[h][:, 1, :])
+            to_z(z_win[3][:, h * HALF : (h + 1) * HALF], y3[h][:])
         nc.sync.dma_start(out=z_own[3][:], in_=z_win[3][:])
         add_results(0, (4, 5), start=True)
         sig[0] = keep.tile([P, GAMES, HALF], F32, name="sig0", tag="res_row0_1")[:]
@@ -309,24 +301,24 @@ def tile_picked_elo8_none_po_kernel(
         sigmoids(7, pieces=((slice(0, 1), last_step), (slice(1, 2), STEP)))
         finish(4)
         finish(5)
-        store_rows(2, PACK, HALF, S)
-        round_columns(HALF, HALF + BLK, nc.scalar.copy)
-        round_columns(HALF + BLK, S, nc.scalar.copy)
+        store_rows(2, 3, 0, S)
 
         with_one = keep.tile([P, 2, HALF], F32, name="with_one")
-        for r in range(2):
-            add_scaled(with_one[:, r, :], sig_last[:, r, 0, :], with_y[:, r, :])
-        add_scaled(rows[:, 2, 0:HALF], sig_last[:, 0, 1, :], with_one[:, 0, :])
-        for cols in (slice(0, BLK), slice(BLK, HALF)):
-            add_scaled(rows[:, 3, cols], sig_last[:, 1, 1, cols], with_one[:, 1, cols])
-        store_rows(2, PACK, 0, HALF)
-        round_columns(0, BLK, nc.vector.tensor_copy)
-        round_columns(BLK, HALF, nc.vector.tensor_copy)
-        quantize(HALF, HALF + BLK)
-        quantize(0, HALF)
-        store_codes(0, HALF)
-        quantize(HALF + BLK, S)
-        store_codes(HALF, S)
+        for h in range(2):
+            add_scaled(with_one[:, h, :], sig_last[:, h, 0, :], with_y[:, h, :])
+        add_scaled(rows[:, 3, 0:HALF], sig_last[:, 0, 1, :], with_one[:, 0, :])
+        for c0 in (0, BLK):
+            add_scaled(rows[:, 3, HALF + c0 : HALF + c0 + BLK], sig_last[:, 1, 1, c0 : c0 + BLK], with_one[:, 1, c0 : c0 + BLK])
+        store_rows(3, PACK, 0, S)
+        round_columns(BLK, HALF, nc.scalar.copy)
+        round_columns(0, BLK, nc.scalar.copy)
+        round_columns(HALF, HALF + BLK, nc.vector.tensor_copy)
+        round_columns(HALF + BLK, S, nc.vector.tensor_copy)
+        quantize(BLK, HALF)
+        quantize(HALF, S)
+        store_codes(BLK, S)
+        quantize(0, BLK)
+        store_codes(0, BLK)
         for q in range(QUADS):
             queue = nc.scalar if q % 2 else nc.sync
             queue.dma_start(

@@ -159,8 +159,8 @@ def tile_picked_elo8_none_po_kernel(
             nc.gpsimd.memset(step, STEP)
         steps.append(STEP)
 
-        z_win = [keep.tile([P, S], F32, name="z_win%d" % t, tag="z_win%d" % t) for t in range(PACK)]
-        z_own = [keep.tile([P, S], F32, name="z_own%d" % t) for t in range(PACK)]
+        z_win = [keep.tile([P, S * (1 + t // 3)], F32, name="z_win%d" % t, tag="z_win%d" % t) for t in range(PACK)]
+        z_own = [z_win[3][:, S : 2 * S] if t == 2 else keep.tile([P, S], F32, name="z_own%d" % t) for t in range(PACK)]
 
         def to_z(out, bank):
             nc.scalar.activation(out=out, in_=bank, func=ACT.Copy, scale=1.0 / STEP)
@@ -230,8 +230,6 @@ def tile_picked_elo8_none_po_kernel(
                 nc.tensor.transpose(backs[k][:, b, :], turned[k][:, b, :], ident[:])
 
         rows = keep.tile([P, PACK, S], F32, name="rows")
-        last_step = rows[:, 3, 0:1]
-        nc.gpsimd.memset(last_step, STEP)
         out_rows = out_0.rearrange("(p t) n -> p t n", t=PACK)
 
         def finish(k):
@@ -270,7 +268,7 @@ def tile_picked_elo8_none_po_kernel(
         add_rating(3)
         for h in range(2):
             to_z(z_win[3][:, h * HALF : (h + 1) * HALF], y3[h][:])
-        nc.sync.dma_start(out=z_own[3][:], in_=z_win[3][:])
+        nc.sync.dma_start(out=z_own[3][:], in_=z_win[3][:, 0:S])
         add_results(0, (4, 5), start=True)
         sig[0] = keep.tile([P, GAMES, HALF], F32, name="sig0", tag="res_row0_1")[:]
         d0 = sigmoids(0)
@@ -288,27 +286,43 @@ def tile_picked_elo8_none_po_kernel(
         leave(1)
         finish(0)
         turn_back(1)
-        for k in range(3, 7):
+        for k in range(3, turned_slots):
             sigmoids(k)
-            if k < turned_slots:
-                add_sigmoids(k)
+            add_sigmoids(k)
             leave(k - 1)
             turn_back(k - 1)
-            if k < turned_slots:
-                finish(k - 2)
+            finish(k - 2)
             if k - 2 in (1, 3):
                 store_rows((k - 2) // 2, (k - 2) // 2 + 1, 0, S)
-        sigmoids(7, pieces=((slice(0, 1), last_step), (slice(1, 2), STEP)))
+
+        def last_tile(l, c0, c1):
+            diffs = all_diffs[:, 1 + l].rearrange("p a c -> p (a c)")[:, c0:c1]
+            nc.vector.tensor_tensor(
+                out=diffs,
+                in0=z_win[3][:].indirect(opp_t[l][:, c0 // GROUP : c1 // GROUP]),
+                in1=z_own[3][:, c0:c1],
+                op=ALU.subtract,
+            )
+            return diffs
+
+        def last_sigmoids(l, c0, c1, diffs, scale=STEP):
+            out = sig_last[:, l].rearrange("p a c -> p (a c)")[:, c0:c1]
+            nc.scalar.activation(out=out, in_=diffs, func=ACT.Sigmoid, scale=scale)
+            return out
+
+        first_game = last_sigmoids(0, 0, S, last_tile(0, 0, S))
+        leave(turned_slots - 1)
+        turn_back(turned_slots - 1)
+        second_early = last_sigmoids(1, 0, HALF, last_tile(1, 0, HALF))
+        with_one = keep.tile([P, S], F32, name="with_one")
+        add_scaled(with_one[:], first_game, with_y[:].rearrange("p h c -> p (h c)"))
+        second_late = last_sigmoids(1, HALF, S, last_tile(1, HALF, S))
         finish(4)
         finish(5)
         store_rows(2, 3, 0, S)
-
-        with_one = keep.tile([P, 2, HALF], F32, name="with_one")
-        for h in range(2):
-            add_scaled(with_one[:, h, :], sig_last[:, h, 0, :], with_y[:, h, :])
-        add_scaled(rows[:, 3, 0:HALF], sig_last[:, 0, 1, :], with_one[:, 0, :])
+        add_scaled(rows[:, 3, 0:HALF], second_early, with_one[:, 0:HALF])
         for c0 in (0, BLK):
-            add_scaled(rows[:, 3, HALF + c0 : HALF + c0 + BLK], sig_last[:, 1, 1, c0 : c0 + BLK], with_one[:, 1, c0 : c0 + BLK])
+            add_scaled(rows[:, 3, HALF + c0 : HALF + c0 + BLK], second_late[:, c0 : c0 + BLK], with_one[:, HALF + c0 : HALF + c0 + BLK])
         store_rows(3, PACK, 0, S)
         round_columns(BLK, HALF, nc.scalar.copy)
         round_columns(0, BLK, nc.scalar.copy)

from contextlib import ExitStack

import concourse.mybir as mybir
from concourse.masks import make_identity

K, T, S, N = 1024, 2048, 512, 512
FLOPS = 2 * K * S * N

F32 = mybir.dt.float32
BF16 = mybir.dt.bfloat16
I32 = mybir.dt.int32
U32 = mybir.dt.uint32
U16 = mybir.dt.uint16
U8 = mybir.dt.uint8
FP8X4 = mybir.dt.float8_e4m3fn_x4
ACT = mybir.ActivationFunctionType
ALU = mybir.AluOpType

P = 128
PACK = 4
PASSES = K // (P * PACK)
QUADS = 4
SCALE_ROWS = 4
GROUP = 16
GAMES = 2
BLK = 128
BLOCKS = S // BLK
HALF = S // 2
STEP = 0.75
DEAL_SPLIT = 84


def tile_picked_elo8_none_po_kernel(
    tc, x_words, x_scales, w1, res1, res2, offs, opp1, opp2, out_0, out_1, out_2
):
    nc = tc.nc
    with ExitStack() as ctx:
        lists = ctx.enter_context(tc.tile_pool(name="lists", bufs=1))
        keep = ctx.enter_context(tc.tile_pool(name="keep", bufs=1))
        psum = ctx.enter_context(tc.psum_pool(name="psum", bufs=1))

        offs_t = lists.tile([P, S // GROUP], U16, name="offs_t")
        opp_t = [lists.tile([P, S // GROUP], U16, name="opp_t%d" % l) for l in range(GAMES)]

        xs_raw = keep.tile([P, PASSES * T], U8, name="xs_raw", align_bytes=64)
        nc.gpsimd.memset(xs_raw[:, 0:T].bitcast(I32), 0)
        nc.vector.memset(xs_raw[:, T:].bitcast(I32), 0)
        xs = keep.tile([P, PASSES * S], U8, name="xs", align_bytes=64)
        nc.vector.memset(xs[:].bitcast(I32), 0)
        ident = keep.tile([P, P], F32, name="ident")
        make_identity(nc, ident[:])
        warm = keep.tile([P, 1], F32, name="warm")
        nc.scalar.activation(out=warm[:], in_=ident[:, 0:1], func=ACT.Sigmoid)

        xw_raw = [keep.tile([P, T], U32, name="xw_raw%d" % g, align_bytes=64) for g in range(PASSES)]
        w_raw = [keep.tile([P, PACK, N], F32, name="w_raw%d" % g) for g in range(PASSES)]
        w_rows = w1.rearrange("(g p j) c -> g p j c", p=P, j=PACK)
        word_rows = [x_words[g].rearrange("p n r -> p (n r)").bitcast(I32) for g in range(PASSES)]

        spread = P // (QUADS * SCALE_ROWS)
        xs_picked = keep.tile([P, PASSES * S], U8, name="xs_picked", align_bytes=64)
        nc.sync.dma_start(out=w_raw[0][:, 0:2, :], in_=w_rows[0][:, 0:2, :])
        nc.sync.dma_start(out=offs_t[:], in_=offs)
        nc.sync.dma_start(
            out=xs_raw[0:P:spread, :].bitcast(I32).rearrange("r (g c) -> r g c", g=PASSES),
            in_=x_scales.bitcast(I32).rearrange("g r c -> r g c"),
        )
        nc.sync.dma_start(out=w_raw[0][:, 2:PACK, :], in_=w_rows[0][:, 2:PACK, :])
        nc.sync.dma_start(out=xw_raw[0][:].bitcast(I32), in_=word_rows[0])
        nc.sync.dma_start(out=w_raw[1][:], in_=w_rows[1])
        for g in range(PASSES):
            nc.vector.tensor_copy(
                out=xs_picked[:, g * S : (g + 1) * S], in_=xs_raw[:, g * T : (g + 1) * T].indirect(offs_t[:])
            )
        for i in range(SCALE_ROWS):
            nc.sync.dma_start(out=xs[i:P:32, :].bitcast(I32), in_=xs_picked[spread * i : P : 32, :].bitcast(I32))
        nc.sync.dma_start(out=xw_raw[1][:].bitcast(I32), in_=word_rows[1])
        res_rows = [res.rearrange("(p t) n -> p t n", t=PACK) for res in (res1, res2)]
        res_row = [[keep.tile([P, S], F32, name="res_row%d_%d" % (l, t), tag="res_row%d_%d" % (l, t)) for t in range(PACK)] for l in range(GAMES)]
        nc.sync.dma_start(out=opp_t[0][:], in_=opp1)
        nc.sync.dma_start(out=opp_t[1][:], in_=opp2)
        for t in (3, 0, 1, 2):
            for l in range(GAMES):
                nc.sync.dma_start(out=res_row[l][t][:], in_=res_rows[l][:, t, :])

        w_bf = [keep.tile([P, PACK * N], BF16, name="w_bf%d" % g, align_bytes=64) for g in range(PASSES)]
        w_codes = [keep.tile([P, N], U32, name="w_codes%d" % g, align_bytes=64) for g in range(PASSES)]
        w_sc = [keep.tile([P, N], U8, name="w_sc%d" % g, align_bytes=64) for g in range(PASSES)]
        xw = [keep.tile([P, S], U32, name="xw%d" % g, align_bytes=64) for g in range(PASSES)]

        def prepare_w(g):
            dealt = w_bf[g][:].rearrange("p (t m j) -> p m t j", t=PACK, j=PACK)
            source = w_raw[g][:].rearrange("p j (m t) -> p m t j", t=PACK)
            nc.vector.tensor_copy(out=dealt[:, 0:DEAL_SPLIT, :, :], in_=source[:, 0:DEAL_SPLIT, :, :])
            nc.scalar.copy(out=dealt[:, DEAL_SPLIT:P, :, :], in_=source[:, DEAL_SPLIT:P, :, :])
            nc.vector.quantize_mx(out=w_codes[g][:].bitcast(FP8X4), scales=w_sc[g][:], in_=w_bf[g][:])

        prepare_w(0)

        def product(out, g, t, c0, c1):
            nc.tensor.matmul_mx(
                out=out,
                lhsT=w_codes[g][:, t * P : (t + 1) * P].bitcast(FP8X4),
                lhsT_scale=w_sc[g][:, t * P : (t + 1) * P],
                rhs=xw[g][:, c0:c1].bitcast(FP8X4),
                rhs_scale=xs[:, g * S + c0 : g * S + c1],
                start=(g == 0),
                stop=(g == PASSES - 1),
            )

        y0 = [psum.tile([P, HALF], F32, name="y0_%d" % h, tag="bank%d" % h) for h in range(2)]
        y1 = psum.tile([P, S], F32, name="y1", tag="bank2")
        nc.vector.tensor_copy(out=xw[0][:], in_=xw_raw[0][:].indirect(offs_t[:]))
        for h in range(2):
            product(y0[h][:], 0, 0, h * HALF, (h + 1) * HALF)
        y2 = psum.tile([P, S], F32, name="y2", tag="bank5")
        y3 = [psum.tile([P, HALF], F32, name="y3_%d" % h, tag="bank%d" % (6 + h)) for h in range(2)]
        for h in range(2):
            product(y3[h][:], 0, 3, h * HALF, (h + 1) * HALF)
        product(y1[:], 0, 1, 0, S)
        product(y2[:], 0, 2, 0, S)
        prepare_w(1)
        for c0, c1 in ((0, HALF), (HALF, S)):
            nc.vector.tensor_copy(out=xw[1][:, c0:c1], in_=xw_raw[1][:].indirect(offs_t[:, c0 // GROUP : c1 // GROUP]))

        for h in range(2):
            product(y0[h][:], 1, 0, h * HALF, (h + 1) * HALF)
            product(y3[h][:], 1, 3, h * HALF, (h + 1) * HALF)
        product(y1[:], 1, 1, 0, S)
        product(y2[:], 1, 2, 0, S)

        def add_scaled(out, term, before, step=STEP):
            nc.vector.scalar_tensor_tensor(out=out, in0=term, scalar=step, in1=before, op0=ALU.mult, op1=ALU.add)

        res_sum = keep.tile([P, S], F32, name="res_sum", tag="z_win3")
        for h in range(2):
            nc.vector.scalar_tensor_tensor(
                out=res_sum[:, h * HALF : (h + 1) * HALF],
                in0=res_row[0][3][:, h * HALF : (h + 1) * HALF],
                scalar=-float(GAMES),
                in1=res_row[1][3][:, h * HALF : (h + 1) * HALF],
                op0=ALU.add,
                op1=ALU.add,
            )
        with_y = keep.tile([P, 2, HALF], F32, name="with_y")
        first_step = keep.tile([P, 1], F32, name="first_step", tag="diffs")
        nc.gpsimd.memset(first_step[:], STEP)
        add_scaled(with_y[:, 0, :], res_sum[:, 0:HALF], y3[0][:], step=first_step[:])
        add_scaled(with_y[:, 1, :], res_sum[:, HALF:S], y3[1][:])

        all_diffs = keep.tile([P, 3, GAMES, HALF], F32, name="diffs", tag="diffs")
        slots = ((0, 0), (0, 1), (1, 0), (1, 1), (2, 0), (2, 1), (3, 0), (3, 1))
        turned_slots = 6
        sig = [None, None] + [keep.tile([P, GAMES, HALF], F32, name="sig%d" % k)[:] for k in range(2, turned_slots)]
        sig_last = keep.tile([P, 2, GAMES, HALF], F32, name="sig_last")
        sig = sig + [sig_last[:, 0], sig_last[:, 1]]
        steps = [sig[k + 2][:, 0, 0:1] for k in range(turned_slots - 1)]
        for step in steps:
            nc.gpsimd.memset(step, STEP)
        steps.append(STEP)

        z_win = [keep.tile([P, S * (1 + t // 3)], F32, name="z_win%d" % t, tag="z_win%d" % t) for t in range(PACK)]
        z_own = [z_win[3][:, S : 2 * S] if t == 2 else keep.tile([P, S], F32, name="z_own%d" % t) for t in range(PACK)]

        def to_z(out, bank):
            nc.scalar.activation(out=out, in_=bank, func=ACT.Copy, scale=1.0 / STEP)

        for h in range(2):
            to_z(z_win[0][:, h * HALF : (h + 1) * HALF], y0[h][:])
            to_z(z_own[0][:, h * HALF : (h + 1) * HALF], y0[h][:])
        to_z(z_win[1][:], y1[:])
        nc.sync.dma_start(out=z_own[1][:, HALF:S], in_=z_win[1][:, HALF:S])
        to_z(z_own[1][:, 0:HALF], y1[:, 0:HALF])

        to_z(z_win[2][:], y2[:])
        nc.sync.dma_start(out=z_own[2][:], in_=z_win[2][:])
        sum_banks = (3, 4, 0, 1, 2, 5)
        sums = [psum.tile([P, 2, P], F32, name="sums%d" % k, tag="bank%d" % sum_banks[k]) for k in range(turned_slots)]

        def add_rows(k, term, start=False, stop=False):
            for b in range(2):
                nc.tensor.matmul(
                    out=sums[k][:, b, :],
                    lhsT=term[:, b * BLK : (b + 1) * BLK],
                    rhs=ident[:],
                    start=start and b == 0,
                    stop=stop and b == 1,
                    is_transpose=True,
                )

        def result(l, t, h):
            return res_row[l][t][:, h * HALF : (h + 1) * HALF]

        def add_rating(k, start=False):
            t, h = slots[k]
            add_rows(k, z_win[t][:, h * HALF : (h + 1) * HALF], start=start)

        def add_results(l, ks, start=False):
            for k in ks:
                t, h = slots[k]
                add_rows(k, result(l, t, h), start=start)

        def sigmoids(k, pieces=((slice(0, GAMES), STEP),)):
            t, h = slots[k]
            diffs = all_diffs[:, (0, 1, 2, 0, 1, 2, 1, 2)[k]]
            for l in range(GAMES):
                nc.vector.tensor_tensor(
                    out=diffs[:, l, :],
                    in0=z_win[t][:].indirect(opp_t[l][:, h * HALF // GROUP : (h + 1) * HALF // GROUP]),
                    in1=z_own[t][:, h * HALF : (h + 1) * HALF],
                    op=ALU.subtract,
                )
            for games, scale in pieces:
                nc.scalar.activation(out=sig[k][:, games, :], in_=diffs[:, games, :], func=ACT.Sigmoid, scale=scale)
            return diffs

        def add_sigmoids(k):
            for l in range(GAMES):
                add_rows(k, sig[k][:, l, :], stop=l == GAMES - 1)

        turned = [keep.tile([P, 2, P], F32, name="turned%d" % k) for k in range(turned_slots)]
        backs = {}

        def leave(k):
            nc.scalar.activation(out=turned[k][:], in_=sums[k][:], func=ACT.Copy, scale=steps[k], bias=-STEP * GAMES)

        def turn_back(k):
            backs[k] = psum.tile([P, 2, BLK], F32, name="back%d" % k, tag="bank%d" % sum_banks[k])
            for b in range(2):
                nc.tensor.transpose(backs[k][:, b, :], turned[k][:, b, :], ident[:])

        rows = keep.tile([P, PACK, S], F32, name="rows")
        out_rows = out_0.rearrange("(p t) n -> p t n", t=PACK)

        def finish(k):
            t, h = slots[k]
            nc.scalar.copy(out=rows[:, t, h * HALF : (h + 1) * HALF], in_=backs[k][:].rearrange("p b c -> p (b c)"))

        def store_rows(t0, t1, c0, c1):
            nc.sync.dma_start(out=out_rows[:, t0:t1, c0:c1], in_=rows[:, t0:t1, c0:c1])

        o_codes = keep.tile([P, S], U32, name="o_codes", align_bytes=64)
        o_sc = keep.tile([P, S], U8, name="o_sc", align_bytes=64)
        out_words = out_1[0].rearrange("p n r -> p (n r)").bitcast(I32)
        rounded = keep.tile([P, S * PACK], BF16, name="rounded", align_bytes=64)

        def round_columns(c0, c1, copy):
            copy(
                out=rounded[:, c0 * PACK : c1 * PACK].rearrange("p (c i t) -> p c t i", i=4, t=PACK),
                in_=rows[:, :, c0:c1].rearrange("p t (c i) -> p c t i", i=4),
            )

        def quantize(c0, c1):
            nc.vector.quantize_mx(
                out=o_codes[:, c0:c1].bitcast(FP8X4), scales=o_sc[:, c0:c1], in_=rounded[:, c0 * PACK : c1 * PACK]
            )

        def store_codes(c0, c1):
            nc.sync.dma_start(out=out_words[:, c0:c1], in_=o_codes[:, c0:c1].bitcast(I32))

        add_rating(0, start=True)
        add_rating(1, start=True)
        for l in range(GAMES):
            add_results(l, (0, 1))
        for l in range(GAMES):
            add_results(l, (2, 3), start=l == 0)
        add_rating(2)
        add_rating(3)
        for h in range(2):
            to_z(z_win[3][:, h * HALF : (h + 1) * HALF], y3[h][:])
        nc.sync.dma_start(out=z_own[3][:], in_=z_win[3][:, 0:S])
        add_results(0, (4, 5), start=True)
        sig[0] = keep.tile([P, GAMES, HALF], F32, name="sig0", tag="res_row0_1")[:]
        d0 = sigmoids(0)
        add_results(1, (4, 5))
        add_sigmoids(0)
        add_rating(4)
        add_rating(5)
        sig[1] = keep.tile([P, GAMES, HALF], F32, name="sig1", tag="res_row1_1")[:]
        sigmoids(1)
        add_sigmoids(1)
        leave(0)
        turn_back(0)
        sigmoids(2)
        add_sigmoids(2)
        leave(1)
        finish(0)
        turn_back(1)
        for k in range(3, turned_slots):
            sigmoids(k)
            add_sigmoids(k)
            leave(k - 1)
            turn_back(k - 1)
            finish(k - 2)
            if k - 2 in (1, 3):
                store_rows((k - 2) // 2, (k - 2) // 2 + 1, 0, S)

        def last_tile(l, c0, c1):
            diffs = all_diffs[:, 1 + l].rearrange("p a c -> p (a c)")[:, c0:c1]
            nc.vector.tensor_tensor(
                out=diffs,
                in0=z_win[3][:].indirect(opp_t[l][:, c0 // GROUP : c1 // GROUP]),
                in1=z_own[3][:, c0:c1],
                op=ALU.subtract,
            )
            return diffs

        def last_sigmoids(l, c0, c1, diffs, scale=STEP):
            out = sig_last[:, l].rearrange("p a c -> p (a c)")[:, c0:c1]
            nc.scalar.activation(out=out, in_=diffs, func=ACT.Sigmoid, scale=scale)
            return out

        first_game = last_sigmoids(0, 0, S, last_tile(0, 0, S))
        leave(turned_slots - 1)
        turn_back(turned_slots - 1)
        second_early = last_sigmoids(1, 0, HALF, last_tile(1, 0, HALF))
        with_one = keep.tile([P, S], F32, name="with_one")
        add_scaled(with_one[:], first_game, with_y[:].rearrange("p h c -> p (h c)"))
        second_late = last_sigmoids(1, HALF, S, last_tile(1, HALF, S))
        finish(4)
        finish(5)
        store_rows(2, 3, 0, S)
        add_scaled(rows[:, 3, 0:HALF], second_early, with_one[:, 0:HALF])
        for c0 in (0, BLK):
            add_scaled(rows[:, 3, HALF + c0 : HALF + c0 + BLK], second_late[:, c0 : c0 + BLK], with_one[:, HALF + c0 : HALF + c0 + BLK])
        store_rows(3, PACK, 0, S)
        round_columns(BLK, HALF, nc.scalar.copy)
        round_columns(0, BLK, nc.scalar.copy)
        round_columns(HALF, HALF + BLK, nc.vector.tensor_copy)
        round_columns(HALF + BLK, S, nc.vector.tensor_copy)
        quantize(BLK, HALF)
        quantize(HALF, S)
        store_codes(BLK, S)
        quantize(0, BLK)
        store_codes(0, BLK)
        for q in range(QUADS):
            queue = nc.scalar if q % 2 else nc.sync
            queue.dma_start(
                out=out_2[0, SCALE_ROWS * q : SCALE_ROWS * (q + 1), :].bitcast(I32),
                in_=o_sc[32 * q : 32 * q + SCALE_ROWS, :].bitcast(I32),
            )
